import numpy as np
import ml_dtypes


def mxq(x, axis, fmt="e4m3"):
    dtype, down = {"e4m3": (ml_dtypes.float8_e4m3fn, 7), "e5m2": (ml_dtypes.float8_e5m2, 14)}[fmt]
    v = np.moveaxis(np.asarray(x, np.float32).astype(ml_dtypes.bfloat16).astype(np.float64), axis, -1)
    blocks = v.reshape(v.shape[:-1] + (-1, 32))
    amax = np.abs(blocks).max(-1, keepdims=True)
    byte = np.maximum(np.where(amax > 0, np.frexp(amax)[1] - 1 + 127, 0) - down, 1)
    scale = np.exp2(byte - 127.0)
    codes = (blocks / scale).astype(np.float32).astype(dtype).astype(np.float64)
    return np.moveaxis((codes * scale).reshape(v.shape), -1, axis)


WIDE = False


def mx_kscale(k, group=512):
    if not WIDE:
        return np.ones(k)
    levels = np.array([18, -18])
    if group != 512:
        return np.exp2(np.random.permutation(np.resize(levels, k // group))).repeat(group)
    if k % 512:
        return np.exp2(np.random.permutation(np.resize(levels, k // 32))).repeat(32)
    a = np.empty((k // 512, 16))
    for p in range(k // 512):
        a[p, :8] = np.random.permutation(np.resize(levels, 8))
        for g in range(8):
            far = levels[np.abs(levels - a[p, g]) >= 10]
            a[p, g + 8] = far[np.random.randint(len(far))]
    return np.exp2(a.ravel()).repeat(32)


def f64(x):
    return np.asarray(x).astype(np.float64)


K, R, M, N = 1024, 128, 512, 512


def setup_inputs():
    n = np.random.standard_normal
    s = mx_kscale(K)[:, None]
    z = mx_kscale(R, 0)
    return {
        "x": (n((K, N)) * s).astype(np.float32),
        "w": (n((K, M)) / np.sqrt(K) / s).astype(np.float32),
        "a": (n((K, R)) / np.sqrt(K) / s * z).astype(np.float32),
        "bb": (n((R, M)) / np.sqrt(R) / z[:, None]).astype(np.float32),
        "b": (0.5 * n((M, 1))).astype(np.float32),
    }


def reference(x, w, a, bb, b):
    xq = mxq(f64(x), 0, "e4m3")
    z = mxq(f64(a), 0, "e4m3").T @ xq
    y = (mxq(f64(w), 0, "e4m3").T @ xq) + (mxq(f64(bb), 0, "e4m3").T @ mxq(z, 0, "e4m3"))
    y = y + f64(b)
    y = np.tanh(y)
    return y

@@ -1,0 +1,269 @@
+from contextlib import ExitStack
+
+import concourse.mybir as mybir
+
+K, R, M, N = 1024, 128, 512, 512
+FLOPS = 2 * K * R * N + 2 * K * M * N + 2 * R * M * N
+
+F32 = mybir.dt.float32
+BF16 = mybir.dt.bfloat16
+U32 = mybir.dt.uint32
+I32 = mybir.dt.int32
+U8 = mybir.dt.uint8
+FP8X4 = mybir.dt.float8_e4m3fn_x4
+ACT = mybir.ActivationFunctionType
+
+P = 128
+PACK = 4
+PASSES = K // (P * PACK)
+QUAD = 32
+TILES = M // P
+CHUNK = 128
+HALF = N // 2
+X_SPLIT = 160
+
+
+def tile_rows_lora_tanh_bias_kernel(tc, x, w, a, bb, b, out):
+    nc = tc.nc
+    with ExitStack() as ctx:
+        keep = ctx.enter_context(tc.tile_pool(name="keep", bufs=1))
+        whole_psum = ctx.enter_context(tc.psum_pool(name="whole_psum", bufs=4))
+        row_psum = ctx.enter_context(tc.psum_pool(name="row_psum", bufs=1))
+        ctx.enter_context(tc.manual_schedule())
+
+        def sb(name, shape, dtype):
+            return keep.tile(shape, dtype, name=name, align_bytes=64)
+
+        def k_rows(c):
+            return slice(c * P * PACK, (c + 1) * P * PACK)
+
+        a_raw = sb("a_raw", [P, PASSES, PACK, R], F32)
+        a_bf = sb("a_bf", [P, PASSES, PACK, QUAD, PACK], BF16)
+        a_codes = sb("a_codes", [P, PASSES * PACK, QUAD], U32)
+        a_scales = sb("a_scales", [P, PASSES * R], U8)
+        a4_codes = sb("a4_codes", [P, PASSES * PACK, TILES, QUAD], U32)
+        a4_scales = sb("a4_scales", [P, PASSES * PACK * P], U8)
+        bb_raw = sb("bb_raw", [P, PACK, P], F32)
+        bb_bf = sb("bb_bf", [P, P, PACK], BF16)
+        bb_codes = sb("bb_codes", [P, P], U32)
+        bb_scales = sb("bb_scales", [P, P], U8)
+        bias = sb("bias", [P, TILES, 1], F32)
+        warm = sb("warm", [P, 8], F32)
+        warm_out = sb("warm_out", [P, 8], F32)
+        hc = [(h, c) for h in range(2) for c in range(PASSES)]
+        tcs = [(t, c) for t in range(TILES) for c in range(PASSES)]
+        x_raw = {k: sb("x_raw%d%d" % k, [P, PACK, HALF], F32) for k in hc}
+        x_bf = {k: sb("x_bf%d%d" % k, [P, HALF, PACK], BF16) for k in hc}
+        x_codes = {k: sb("x_codes%d%d" % k, [P, HALF], U32) for k in hc}
+        x_scales = {k: sb("x_scales%d%d" % k, [P, HALF], U8) for k in hc}
+        w_raw = {k: sb("w_raw%d%d" % k, [P, PACK, P], F32) for k in tcs}
+        w_bf = {k: sb("w_bf%d%d" % k, [P, P, PACK], BF16) for k in tcs}
+        w_codes = {k: sb("w_codes%d%d" % k, [P, P], U32) for k in tcs}
+        w_scales = {k: sb("w_scales%d%d" % k, [P, P], U8) for k in tcs}
+        z_bf = [sb("z_bf%d" % i, [P, CHUNK, PACK], BF16) for i in range(4)]
+        z_codes = [sb("z_codes%d" % i, [P, CHUNK], U32) for i in range(4)]
+        z_scales = [sb("z_scales%d" % i, [P, CHUNK], U8) for i in range(4)]
+        th = [(t, h) for t in range(TILES) for h in range(2)]
+        low = {k: sb("low%d%d" % k, [P, HALF], F32) for k in th}
+        pre = {k: sb("pre%d%d" % k, [P, HALF], F32) for k in th}
+        res = {k: sb("res%d%d" % k, [P, HALF], F32) for k in th}
+        low_bank = [row_psum.tile([P, N], F32, name="low_bank%d" % t) for t in range(TILES)]
+        z_bank = {}
+        y_bank = {}
+
+        def copy(eng, out_ap, in_ap):
+            if eng == "v":
+                nc.vector.tensor_copy(out=out_ap, in_=in_ap)
+            else:
+                nc.scalar.copy(out=out_ap, in_=in_ap)
+
+        def weave(eng, dst, src, lo, hi):
+            copy(eng,
+                 dst[:, lo:hi, :].rearrange("p (c i) j -> p c j i", i=4),
+                 src[:, :, lo:hi].rearrange("p j (c i) -> p c j i", i=4))
+
+        def quantize(codes, scales, src):
+            nc.vector.quantize_mx(out=codes.bitcast(FP8X4), scales=scales, in_=src)
+
+        def load_x(h, c):
+            nc.sync.dma_start(out=x_raw[h, c][:], in_=x[k_rows(c), h * HALF:(h + 1) * HALF].rearrange("(p j) n -> p j n", j=PACK))
+
+        def load_w(t, c):
+            nc.sync.dma_start(out=w_raw[t, c][:], in_=w[k_rows(c), t * P:(t + 1) * P].rearrange("(p j) m -> p j m", j=PACK))
+
+        def weave_a(eng, c):
+            copy(eng, a_bf[:, c, :, :, :], a_raw[:, c, :, :].rearrange("p j (i s) -> p s i j", s=PACK))
+
+        def weave_x(eng, h, c):
+            lo, hi = (0, X_SPLIT) if eng == "v" else (X_SPLIT, HALF)
+            weave(eng, x_bf[h, c], x_raw[h, c], lo, hi)
+
+        def quant_x(h, c):
+            quantize(x_codes[h, c][:], x_scales[h, c][:], x_bf[h, c][:].rearrange("p n j -> p (n j)"))
+
+        def weave_w(eng, t, c):
+            weave(eng, w_bf[t, c], w_raw[t, c], 0, P)
+
+        def quant_w(t, c):
+            quantize(w_codes[t, c][:], w_scales[t, c][:], w_bf[t, c][:].rearrange("p n j -> p (n j)"))
+
+        def x_cols(i, c):
+            h, cols = i // 2, slice((i % 2) * CHUNK, (i % 2 + 1) * CHUNK)
+            return x_codes[h, c][:, cols].bitcast(FP8X4), x_scales[h, c][:, cols]
+
+        def mm_z(i):
+            z_bank[i] = whole_psum.tile([P, PACK, CHUNK], F32, name="z_bank%d" % i, tag="whole")
+            for s in range(PACK):
+                for c in range(PASSES):
+                    g = c * PACK + s
+                    rhs, rhs_scale = x_cols(i, c)
+                    nc.tensor.matmul_mx(
+                        out=z_bank[i][:, s, :],
+                        lhsT=a4_codes[:, g, :, :].rearrange("p q i -> p (q i)").bitcast(FP8X4),
+                        lhsT_scale=a4_scales[:, g * P:(g + 1) * P],
+                        rhs=rhs, rhs_scale=rhs_scale, start=(c == 0), stop=(c == PASSES - 1))
+
+        def evac_z(eng, i):
+            copy(eng, z_bf[i][:], z_bank[i][:].rearrange("p s n -> p n s"))
+
+        def quant_z(i):
+            quantize(z_codes[i][:], z_scales[i][:], z_bf[i][:].rearrange("p n j -> p (n j)"))
+
+        def mm_low(h):
+            for i in (2 * h, 2 * h + 1):
+                for t in range(TILES):
+                    rows = slice(QUAD * t, QUAD * (t + 1))
+                    nc.tensor.matmul_mx(
+                        out=low_bank[t][:, i * CHUNK:(i + 1) * CHUNK],
+                        lhsT=bb_codes[rows, :].bitcast(FP8X4), lhsT_scale=bb_scales[rows, :],
+                        rhs=z_codes[i][rows, :].bitcast(FP8X4), rhs_scale=z_scales[i][rows, :],
+                        start=True, stop=True)
+
+        def evac_low(eng, t, h):
+            copy(eng, low[t, h][:], low_bank[t][:, h * HALF:(h + 1) * HALF])
+
+        def mm_y(t, h):
+            y_bank[t, h] = whole_psum.tile([P, HALF], F32, name="y_bank%d%d" % (t, h), tag="whole")
+            for i in (2 * h, 2 * h + 1):
+                for c in range(PASSES):
+                    rhs, rhs_scale = x_cols(i, c)
+                    nc.tensor.matmul_mx(
+                        out=y_bank[t, h][:, (i % 2) * CHUNK:(i % 2 + 1) * CHUNK],
+                        lhsT=w_codes[t, c][:].bitcast(FP8X4), lhsT_scale=w_scales[t, c][:],
+                        rhs=rhs, rhs_scale=rhs_scale, start=(c == 0), stop=(c == PASSES - 1))
+
+        def add(t, h):
+            nc.vector.tensor_tensor(out=pre[t, h][:], in0=y_bank[t, h][:], in1=low[t, h][:], op=mybir.AluOpType.add)
+
+        def finish(t, h):
+            nc.scalar.activation(out=res[t, h][:], in_=pre[t, h][:], func=ACT.Tanh, bias=bias[:, t, :])
+            nc.sync.dma_start(out=out[t * P:(t + 1) * P, h * HALF:(h + 1) * HALF], in_=res[t, h][:])
+
+        def load_bb():
+            for t in range(TILES):
+                nc.sync.dma_start(out=bb_raw[QUAD * t:QUAD * (t + 1), :, :],
+                                  in_=bb[:, t * P:(t + 1) * P].rearrange("(p j) m -> p j m", j=PACK))
+
+        def load_bias():
+            with nc.allow_non_contiguous_dma(reason="one bias a partition"):
+                nc.sync.dma_start(out=bias[:], in_=b.rearrange("(t p) o -> p t o", p=P))
+
+        def load_a():
+            nc.sync.dma_start(out=a_raw[:].rearrange("p c j r -> p c (j r)"), in_=a.rearrange("(c p j) r -> p c (j r)", c=PASSES, j=PACK))
+
+        nc.gpsimd.memset(warm[:], 0.0)
+        nc.gpsimd.memset(a_scales[:].bitcast(I32), 0)
+        nc.scalar.activation(out=warm_out[:], in_=warm[:], func=ACT.Tanh)
+
+        load_a()
+        load_x(0, 0)
+        load_x(0, 1)
+        load_bb()
+        load_x(1, 0)
+        load_x(1, 1)
+        load_bias()
+        for t, c in tcs:
+            load_w(t, c)
+        weave_a("v", 0)
+        weave_a("s", 1)
+        quantize(a_codes[:].rearrange("p g i -> p (g i)"), a_scales[:], a_bf[:].rearrange("p c s i j -> p (c s i j)"))
+        weave_x("s", 0, 0)
+        weave_x("v", 0, 0)
+        nc.vector.tensor_copy(out=a4_codes[:].bitcast(I32), in_=a_codes[:].bitcast(I32).unsqueeze(2).to_broadcast([P, PASSES * PACK, TILES, QUAD]))
+        quant_x(0, 0)
+        nc.vector.tensor_copy(
+            out=a4_scales[:].bitcast(I32).rearrange("p (g q i) -> p g q i", q=TILES, i=QUAD // 4),
+            in_=a_scales[:].bitcast(I32).rearrange("p (g i) -> p g i", i=QUAD // 4).unsqueeze(2).to_broadcast([P, PASSES * PACK, TILES, QUAD // 4]))
+        weave_x("s", 0, 1)
+        weave_x("v", 0, 1)
+        weave("s", bb_bf, bb_raw, 0, P)
+        quant_x(0, 1)
+        mm_z(0)
+        mm_z(1)
+        weave_x("s", 1, 0)
+        weave_x("v", 1, 0)
+        quantize(bb_codes[:], bb_scales[:], bb_bf[:].rearrange("p n j -> p (n j)"))
+        evac_z("s", 0)
+        quant_x(1, 0)
+        weave_x("s", 1, 1)
+        weave_x("v", 1, 1)
+        quant_z(0)
+        quant_x(1, 1)
+        evac_z("s", 1)
+        mm_z(2)
+        mm_z(3)
+        weave_w("v", 0, 0)
+        quant_z(1)
+        mm_low(0)
+        weave_w("v", 0, 1)
+        quant_w(0, 0)
+        evac_z("s", 2)
+        evac_z("s", 3)
+        quant_w(0, 1)
+        mm_y(0, 0)
+        quant_z(2)
+        weave_w("v", 1, 0)
+        quant_z(3)
+        mm_low(1)
+        mm_y(0, 1)
+        weave_w("v", 1, 1)
+        quant_w(1, 0)
+        evac_low("s", 0, 0)
+        evac_low("s", 0, 1)
+        quant_w(1, 1)
+        mm_y(1, 0)
+        mm_y(1, 1)
+        weave_w("v", 2, 0)
+        add(0, 0)
+        evac_low("s", 1, 0)
+        evac_low("s", 1, 1)
+        weave_w("v", 2, 1)
+        quant_w(2, 0)
+        add(0, 1)
+        finish(0, 0)
+        quant_w(2, 1)
+        mm_y(2, 0)
+        finish(0, 1)
+        evac_low("s", 2, 0)
+        evac_low("s", 2, 1)
+        add(1, 0)
+        weave_w("v", 3, 0)
+        add(1, 1)
+        mm_y(2, 1)
+        finish(1, 0)
+        finish(1, 1)
+        evac_low("s", 3, 0)
+        evac_low("s", 3, 1)
+        weave_w("v", 3, 1)
+        quant_w(3, 0)
+        add(2, 0)
+        quant_w(3, 1)
+        mm_y(3, 0)
+        mm_y(3, 1)
+        add(2, 1)
+        finish(2, 0)
+        finish(2, 1)
+        add(3, 0)
+        add(3, 1)
+        finish(3, 0)
+        finish(3, 1)

@@ -19,8 +19,7 @@ PASSES = K // (P * PACK)
 QUAD = 32
 TILES = M // P
 CHUNK = 128
-HALF = N // 2
-X_SPLIT = 160
+CHUNKS = N // CHUNK
 
 
 def tile_rows_lora_tanh_bias_kernel(tc, x, w, a, bb, b, out):
@@ -37,6 +36,9 @@ def tile_rows_lora_tanh_bias_kernel(tc, x, w, a, bb, b, out):
         def k_rows(c):
             return slice(c * P * PACK, (c + 1) * P * PACK)
 
+        def cols(lo, hi):
+            return slice(lo * CHUNK, hi * CHUNK)
+
         a_raw = sb("a_raw", [P, PASSES, PACK, R], F32)
         a_bf = sb("a_bf", [P, PASSES, PACK, QUAD, PACK], BF16)
         a_codes = sb("a_codes", [P, PASSES * PACK, QUAD], U32)
@@ -50,23 +52,21 @@ def tile_rows_lora_tanh_bias_kernel(tc, x, w, a, bb, b, out):
         bias = sb("bias", [P, TILES, 1], F32)
         warm = sb("warm", [P, 8], F32)
         warm_out = sb("warm_out", [P, 8], F32)
-        hc = [(h, c) for h in range(2) for c in range(PASSES)]
         tcs = [(t, c) for t in range(TILES) for c in range(PASSES)]
-        x_raw = {k: sb("x_raw%d%d" % k, [P, PACK, HALF], F32) for k in hc}
-        x_bf = {k: sb("x_bf%d%d" % k, [P, HALF, PACK], BF16) for k in hc}
-        x_codes = {k: sb("x_codes%d%d" % k, [P, HALF], U32) for k in hc}
-        x_scales = {k: sb("x_scales%d%d" % k, [P, HALF], U8) for k in hc}
-        w_raw = {k: sb("w_raw%d%d" % k, [P, PACK, P], F32) for k in tcs}
+        x_raw = [sb("x_raw%d" % c, [P, PACK, N], F32) for c in range(PASSES)]
+        x_bf = [sb("x_bf%d" % c, [P, N, PACK], BF16) for c in range(PASSES)]
+        x_codes = [sb("x_codes%d" % c, [P, N], U32) for c in range(PASSES)]
+        x_scales = [sb("x_scales%d" % c, [P, N], U8) for c in range(PASSES)]
+        w_raw = {}
         w_bf = {k: sb("w_bf%d%d" % k, [P, P, PACK], BF16) for k in tcs}
         w_codes = {k: sb("w_codes%d%d" % k, [P, P], U32) for k in tcs}
         w_scales = {k: sb("w_scales%d%d" % k, [P, P], U8) for k in tcs}
-        z_bf = [sb("z_bf%d" % i, [P, CHUNK, PACK], BF16) for i in range(4)]
-        z_codes = [sb("z_codes%d" % i, [P, CHUNK], U32) for i in range(4)]
-        z_scales = [sb("z_scales%d" % i, [P, CHUNK], U8) for i in range(4)]
-        th = [(t, h) for t in range(TILES) for h in range(2)]
-        low = {k: sb("low%d%d" % k, [P, HALF], F32) for k in th}
-        pre = {k: sb("pre%d%d" % k, [P, HALF], F32) for k in th}
-        res = {k: sb("res%d%d" % k, [P, HALF], F32) for k in th}
+        z_bf = [sb("z_bf%d" % i, [P, CHUNK, PACK], BF16) for i in range(CHUNKS)]
+        z_codes = [sb("z_codes%d" % i, [P, CHUNK], U32) for i in range(CHUNKS)]
+        z_scales = [sb("z_scales%d" % i, [P, CHUNK], U8) for i in range(CHUNKS)]
+        low = [sb("low%d" % t, [P, N], F32) for t in range(TILES)]
+        pre = [sb("pre%d" % t, [P, N], F32) for t in range(TILES)]
+        res = [sb("res%d" % t, [P, N], F32) for t in range(TILES)]
         low_bank = [row_psum.tile([P, N], F32, name="low_bank%d" % t) for t in range(TILES)]
         z_bank = {}
         y_bank = {}
@@ -77,193 +77,219 @@ def tile_rows_lora_tanh_bias_kernel(tc, x, w, a, bb, b, out):
             else:
                 nc.scalar.copy(out=out_ap, in_=in_ap)
 
-        def weave(eng, dst, src, lo, hi):
-            copy(eng,
-                 dst[:, lo:hi, :].rearrange("p (c i) j -> p c j i", i=4),
-                 src[:, :, lo:hi].rearrange("p j (c i) -> p c j i", i=4))
+        def weave(eng, dst, src):
+            copy(eng, dst.rearrange("p (c i) j -> p c j i", i=4), src.rearrange("p j (c i) -> p c j i", i=4))
 
         def quantize(codes, scales, src):
-            nc.vector.quantize_mx(out=codes.bitcast(FP8X4), scales=scales, in_=src)
+            nc.vector.quantize_mx(out=codes.bitcast(FP8X4), scales=scales, in_=src.rearrange("p n j -> p (n j)"))
 
-        def load_x(h, c):
-            nc.sync.dma_start(out=x_raw[h, c][:], in_=x[k_rows(c), h * HALF:(h + 1) * HALF].rearrange("(p j) n -> p j n", j=PACK))
+        def La():
+            nc.sync.dma_start(out=a_raw[:].rearrange("p c j r -> p c (j r)"), in_=a.rearrange("(c p j) r -> p c (j r)", c=PASSES, j=PACK))
 
-        def load_w(t, c):
-            nc.sync.dma_start(out=w_raw[t, c][:], in_=w[k_rows(c), t * P:(t + 1) * P].rearrange("(p j) m -> p j m", j=PACK))
+        def Lx(c):
+            nc.sync.dma_start(out=x_raw[c][:], in_=x[k_rows(c), :].rearrange("(p j) n -> p j n", j=PACK))
 
-        def weave_a(eng, c):
-            copy(eng, a_bf[:, c, :, :, :], a_raw[:, c, :, :].rearrange("p j (i s) -> p s i j", s=PACK))
+        def Lb(t):
+            nc.sync.dma_start(out=bb_raw[QUAD * t:QUAD * (t + 1), :, :],
+                              in_=bb[:, t * P:(t + 1) * P].rearrange("(p j) m -> p j m", j=PACK))
 
-        def weave_x(eng, h, c):
-            lo, hi = (0, X_SPLIT) if eng == "v" else (X_SPLIT, HALF)
-            weave(eng, x_bf[h, c], x_raw[h, c], lo, hi)
-
-        def quant_x(h, c):
-            quantize(x_codes[h, c][:], x_scales[h, c][:], x_bf[h, c][:].rearrange("p n j -> p (n j)"))
-
-        def weave_w(eng, t, c):
-            weave(eng, w_bf[t, c], w_raw[t, c], 0, P)
-
-        def quant_w(t, c):
-            quantize(w_codes[t, c][:], w_scales[t, c][:], w_bf[t, c][:].rearrange("p n j -> p (n j)"))
-
-        def x_cols(i, c):
-            h, cols = i // 2, slice((i % 2) * CHUNK, (i % 2 + 1) * CHUNK)
-            return x_codes[h, c][:, cols].bitcast(FP8X4), x_scales[h, c][:, cols]
-
-        def mm_z(i):
-            z_bank[i] = whole_psum.tile([P, PACK, CHUNK], F32, name="z_bank%d" % i, tag="whole")
-            for s in range(PACK):
-                for c in range(PASSES):
-                    g = c * PACK + s
-                    rhs, rhs_scale = x_cols(i, c)
-                    nc.tensor.matmul_mx(
-                        out=z_bank[i][:, s, :],
-                        lhsT=a4_codes[:, g, :, :].rearrange("p q i -> p (q i)").bitcast(FP8X4),
-                        lhsT_scale=a4_scales[:, g * P:(g + 1) * P],
-                        rhs=rhs, rhs_scale=rhs_scale, start=(c == 0), stop=(c == PASSES - 1))
-
-        def evac_z(eng, i):
-            copy(eng, z_bf[i][:], z_bank[i][:].rearrange("p s n -> p n s"))
-
-        def quant_z(i):
-            quantize(z_codes[i][:], z_scales[i][:], z_bf[i][:].rearrange("p n j -> p (n j)"))
-
-        def mm_low(h):
-            for i in (2 * h, 2 * h + 1):
-                for t in range(TILES):
-                    rows = slice(QUAD * t, QUAD * (t + 1))
-                    nc.tensor.matmul_mx(
-                        out=low_bank[t][:, i * CHUNK:(i + 1) * CHUNK],
-                        lhsT=bb_codes[rows, :].bitcast(FP8X4), lhsT_scale=bb_scales[rows, :],
-                        rhs=z_codes[i][rows, :].bitcast(FP8X4), rhs_scale=z_scales[i][rows, :],
-                        start=True, stop=True)
-
-        def evac_low(eng, t, h):
-            copy(eng, low[t, h][:], low_bank[t][:, h * HALF:(h + 1) * HALF])
-
-        def mm_y(t, h):
-            y_bank[t, h] = whole_psum.tile([P, HALF], F32, name="y_bank%d%d" % (t, h), tag="whole")
-            for i in (2 * h, 2 * h + 1):
-                for c in range(PASSES):
-                    rhs, rhs_scale = x_cols(i, c)
-                    nc.tensor.matmul_mx(
-                        out=y_bank[t, h][:, (i % 2) * CHUNK:(i % 2 + 1) * CHUNK],
-                        lhsT=w_codes[t, c][:].bitcast(FP8X4), lhsT_scale=w_scales[t, c][:],
-                        rhs=rhs, rhs_scale=rhs_scale, start=(c == 0), stop=(c == PASSES - 1))
-
-        def add(t, h):
-            nc.vector.tensor_tensor(out=pre[t, h][:], in0=y_bank[t, h][:], in1=low[t, h][:], op=mybir.AluOpType.add)
-
-        def finish(t, h):
-            nc.scalar.activation(out=res[t, h][:], in_=pre[t, h][:], func=ACT.Tanh, bias=bias[:, t, :])
-            nc.sync.dma_start(out=out[t * P:(t + 1) * P, h * HALF:(h + 1) * HALF], in_=res[t, h][:])
-
-        def load_bb():
-            for t in range(TILES):
-                nc.sync.dma_start(out=bb_raw[QUAD * t:QUAD * (t + 1), :, :],
-                                  in_=bb[:, t * P:(t + 1) * P].rearrange("(p j) m -> p j m", j=PACK))
-
-        def load_bias():
+        def Lbias():
             with nc.allow_non_contiguous_dma(reason="one bias a partition"):
                 nc.sync.dma_start(out=bias[:], in_=b.rearrange("(t p) o -> p t o", p=P))
 
-        def load_a():
-            nc.sync.dma_start(out=a_raw[:].rearrange("p c j r -> p c (j r)"), in_=a.rearrange("(c p j) r -> p c (j r)", c=PASSES, j=PACK))
+        def Lw(c, lo, hi):
+            raw = sb("w_raw%d%d" % (c, lo), [P, PACK, (hi - lo) * P], F32)
+            nc.sync.dma_start(out=raw[:], in_=w[k_rows(c), lo * P:hi * P].rearrange("(p j) m -> p j m", j=PACK))
+            for t in range(lo, hi):
+                w_raw[t, c] = raw[:, :, (t - lo) * P:(t - lo + 1) * P]
+
+        def ia(eng, c):
+            copy(eng, a_bf[:, c, :, :, :], a_raw[:, c, :, :].rearrange("p j (i s) -> p s i j", s=PACK))
+
+        def qa():
+            quantize(a_codes[:].rearrange("p g i -> p (g i)"), a_scales[:], a_bf[:].rearrange("p c s i j -> p (c s i) j"))
+
+        def ca():
+            nc.vector.tensor_copy(out=a4_codes[:].bitcast(I32),
+                                  in_=a_codes[:].bitcast(I32).unsqueeze(2).to_broadcast([P, PASSES * PACK, TILES, QUAD]))
+
+        def cs():
+            nc.vector.tensor_copy(
+                out=a4_scales[:].bitcast(I32).rearrange("p (g q i) -> p g q i", q=TILES, i=QUAD // 4),
+                in_=a_scales[:].bitcast(I32).rearrange("p (g i) -> p g i", i=QUAD // 4).unsqueeze(2).to_broadcast([P, PASSES * PACK, TILES, QUAD // 4]))
+
+        def ix(eng, c, i):
+            weave(eng, x_bf[c][:, cols(i, i + 1), :], x_raw[c][:, :, cols(i, i + 1)])
+
+        def qx(c, lo, hi):
+            quantize(x_codes[c][:, cols(lo, hi)], x_scales[c][:, cols(lo, hi)], x_bf[c][:, cols(lo, hi), :])
+
+        def ib(eng):
+            weave(eng, bb_bf[:], bb_raw[:])
+
+        def qb():
+            quantize(bb_codes[:], bb_scales[:], bb_bf[:])
+
+        def iw(eng, t, c):
+            weave(eng, w_bf[t, c][:], w_raw[t, c])
+
+        def qw(t, c):
+            quantize(w_codes[t, c][:], w_scales[t, c][:], w_bf[t, c][:])
+
+        def z_pass(dst, s, i, c, start, stop):
+            g = c * PACK + s
+            nc.tensor.matmul_mx(
+                out=dst,
+                lhsT=a4_codes[:, g, :, :].rearrange("p q i -> p (q i)").bitcast(FP8X4),
+                lhsT_scale=a4_scales[:, g * P:(g + 1) * P],
+                rhs=x_codes[c][:, cols(i, i + 1)].bitcast(FP8X4), rhs_scale=x_scales[c][:, cols(i, i + 1)],
+                start=start, stop=stop)
+
+        def wu(count):
+            scratch = whole_psum.tile([P, PACK, CHUNK], F32, name="scratch", tag="whole")
+            for r in range(count):
+                z_pass(scratch[:, r % PACK, :], r % PACK, 0, 0, True, True)
+
+        def mz(i):
+            z_bank[i] = whole_psum.tile([P, PACK, CHUNK], F32, name="z_bank%d" % i, tag="whole")
+            for s in range(PACK):
+                for c in range(PASSES):
+                    z_pass(z_bank[i][:, s, :], s, i, c, c == 0, c == PASSES - 1)
+
+        def ez(eng, i):
+            copy(eng, z_bf[i][:], z_bank[i][:].rearrange("p s n -> p n s"))
+
+        def qz(i):
+            quantize(z_codes[i][:], z_scales[i][:], z_bf[i][:])
+
+        def ml(i):
+            for t in range(TILES):
+                rows = slice(QUAD * t, QUAD * (t + 1))
+                nc.tensor.matmul_mx(
+                    out=low_bank[t][:, cols(i, i + 1)],
+                    lhsT=bb_codes[rows, :].bitcast(FP8X4), lhsT_scale=bb_scales[rows, :],
+                    rhs=z_codes[i][rows, :].bitcast(FP8X4), rhs_scale=z_scales[i][rows, :],
+                    start=True, stop=True)
+
+        def el(eng, t, lo, hi):
+            copy(eng, low[t][:, cols(lo, hi)], low_bank[t][:, cols(lo, hi)])
+
+        def my(t, lo, hi):
+            y_bank[t, lo] = whole_psum.tile([P, (hi - lo) * CHUNK], F32, name="y_bank%d%d" % (t, lo), tag="whole")
+            for i in range(lo, hi):
+                for c in range(PASSES):
+                    nc.tensor.matmul_mx(
+                        out=y_bank[t, lo][:, cols(i - lo, i - lo + 1)],
+                        lhsT=w_codes[t, c][:].bitcast(FP8X4), lhsT_scale=w_scales[t, c][:],
+                        rhs=x_codes[c][:, cols(i, i + 1)].bitcast(FP8X4), rhs_scale=x_scales[c][:, cols(i, i + 1)],
+                        start=(c == 0), stop=(c == PASSES - 1))
+
+        def ad(t, lo, hi):
+            nc.vector.tensor_tensor(out=pre[t][:, cols(lo, hi)], in0=y_bank[t, lo][:], in1=low[t][:, cols(lo, hi)],
+                                    op=mybir.AluOpType.add)
+
+        def th(t, lo, hi):
+            nc.scalar.activation(out=res[t][:, cols(lo, hi)], in_=pre[t][:, cols(lo, hi)], func=ACT.Tanh, bias=bias[:, t, :])
+
+        def St(t, lo, hi):
+            nc.sync.dma_start(out=out[t * P:(t + 1) * P, cols(lo, hi)], in_=res[t][:, cols(lo, hi)])
+
+        def tbl():
+            nc.scalar.activation(out=warm_out[:], in_=warm[:], func=ACT.Tanh)
 
         nc.gpsimd.memset(warm[:], 0.0)
         nc.gpsimd.memset(a_scales[:].bitcast(I32), 0)
-        nc.scalar.activation(out=warm_out[:], in_=warm[:], func=ACT.Tanh)
-
-        load_a()
-        load_x(0, 0)
-        load_x(0, 1)
-        load_bb()
-        load_x(1, 0)
-        load_x(1, 1)
-        load_bias()
-        for t, c in tcs:
-            load_w(t, c)
-        weave_a("v", 0)
-        weave_a("s", 1)
-        quantize(a_codes[:].rearrange("p g i -> p (g i)"), a_scales[:], a_bf[:].rearrange("p c s i j -> p (c s i j)"))
-        weave_x("s", 0, 0)
-        weave_x("v", 0, 0)
-        nc.vector.tensor_copy(out=a4_codes[:].bitcast(I32), in_=a_codes[:].bitcast(I32).unsqueeze(2).to_broadcast([P, PASSES * PACK, TILES, QUAD]))
-        quant_x(0, 0)
-        nc.vector.tensor_copy(
-            out=a4_scales[:].bitcast(I32).rearrange("p (g q i) -> p g q i", q=TILES, i=QUAD // 4),
-            in_=a_scales[:].bitcast(I32).rearrange("p (g i) -> p g i", i=QUAD // 4).unsqueeze(2).to_broadcast([P, PASSES * PACK, TILES, QUAD // 4]))
-        weave_x("s", 0, 1)
-        weave_x("v", 0, 1)
-        weave("s", bb_bf, bb_raw, 0, P)
-        quant_x(0, 1)
-        mm_z(0)
-        mm_z(1)
-        weave_x("s", 1, 0)
-        weave_x("v", 1, 0)
-        quantize(bb_codes[:], bb_scales[:], bb_bf[:].rearrange("p n j -> p (n j)"))
-        evac_z("s", 0)
-        quant_x(1, 0)
-        weave_x("s", 1, 1)
-        weave_x("v", 1, 1)
-        quant_z(0)
-        quant_x(1, 1)
-        evac_z("s", 1)
-        mm_z(2)
-        mm_z(3)
-        weave_w("v", 0, 0)
-        quant_z(1)
-        mm_low(0)
-        weave_w("v", 0, 1)
-        quant_w(0, 0)
-        evac_z("s", 2)
-        evac_z("s", 3)
-        quant_w(0, 1)
-        mm_y(0, 0)
-        quant_z(2)
-        weave_w("v", 1, 0)
-        quant_z(3)
-        mm_low(1)
-        mm_y(0, 1)
-        weave_w("v", 1, 1)
-        quant_w(1, 0)
-        evac_low("s", 0, 0)
-        evac_low("s", 0, 1)
-        quant_w(1, 1)
-        mm_y(1, 0)
-        mm_y(1, 1)
-        weave_w("v", 2, 0)
-        add(0, 0)
-        evac_low("s", 1, 0)
-        evac_low("s", 1, 1)
-        weave_w("v", 2, 1)
-        quant_w(2, 0)
-        add(0, 1)
-        finish(0, 0)
-        quant_w(2, 1)
-        mm_y(2, 0)
-        finish(0, 1)
-        evac_low("s", 2, 0)
-        evac_low("s", 2, 1)
-        add(1, 0)
-        weave_w("v", 3, 0)
-        add(1, 1)
-        mm_y(2, 1)
-        finish(1, 0)
-        finish(1, 1)
-        evac_low("s", 3, 0)
-        evac_low("s", 3, 1)
-        weave_w("v", 3, 1)
-        quant_w(3, 0)
-        add(2, 0)
-        quant_w(3, 1)
-        mm_y(3, 0)
-        mm_y(3, 1)
-        add(2, 1)
-        finish(2, 0)
-        finish(2, 1)
-        add(3, 0)
-        add(3, 1)
-        finish(3, 0)
-        finish(3, 1)
+        La()
+        tbl()
+        Lx(0)
+        Lx(1)
+        Lb(0)
+        Lb(2)
+        Lb(1)
+        Lb(3)
+        Lw(0, 0, 2)
+        Lw(1, 0, 2)
+        ia("v", 0)
+        ia("s", 1)
+        qa()
+        ca()
+        cs()
+        Lw(0, 2, 4)
+        ix("v", 0, 0)
+        ix("s", 0, 2)
+        ix("v", 0, 1)
+        ix("s", 0, 3)
+        qx(0, 0, 2)
+        qx(0, 2, 4)
+        wu(14)
+        Lw(1, 2, 4)
+        ix("v", 1, 0)
+        ix("s", 1, 2)
+        Lbias()
+        ix("v", 1, 1)
+        ix("s", 1, 3)
+        qx(1, 0, 1)
+        qx(1, 1, 2)
+        qx(1, 2, 3)
+        mz(0)
+        ib("s")
+        qx(1, 3, 4)
+        mz(1)
+        ez("s", 0)
+        qb()
+        mz(2)
+        iw("v", 0, 0)
+        ez("s", 1)
+        qz(0)
+        mz(3)
+        iw("v", 1, 0)
+        ez("s", 2)
+        qw(0, 0)
+        qz(1)
+        ml(0)
+        qw(1, 0)
+        ez("s", 3)
+        ml(1)
+        iw("v", 0, 1)
+        qz(2)
+        iw("v", 1, 1)
+        ml(2)
+        qz(3)
+        qw(0, 1)
+        qw(1, 1)
+        ml(3)
+        iw("v", 2, 0)
+        my(0, 0, 4)
+        iw("v", 3, 0)
+        el("s", 0, 0, 4)
+        qw(2, 0)
+        my(1, 0, 4)
+        qw(3, 0)
+        el("s", 1, 0, 4)
+        ad(0, 0, 4)
+        el("s", 2, 0, 4)
+        iw("v", 2, 1)
+        iw("v", 3, 1)
+        th(0, 0, 4)
+        qw(2, 1)
+        ad(1, 0, 4)
+        el("s", 3, 0, 4)
+        my(2, 0, 2)
+        St(0, 0, 4)
+        my(2, 2, 4)
+        qw(3, 1)
+        ad(2, 0, 2)
+        th(1, 0, 4)
+        my(3, 0, 2)
+        ad(2, 2, 4)
+        my(3, 2, 4)
+        th(2, 0, 2)
+        ad(3, 0, 2)
+        St(1, 0, 4)
+        th(2, 2, 4)
+        ad(3, 2, 4)
+        th(3, 0, 2)
+        St(2, 0, 4)
+        th(3, 2, 4)
+        St(3, 0, 2)
+        St(3, 2, 4)

@@ -19,6 +19,7 @@ PASSES = K // (P * PACK)
 QUAD = 32
 TILES = M // P
 CHUNK = 128
+RUN = 2
 CHUNKS = N // CHUNK
 
 
@@ -49,11 +50,12 @@ def tile_rows_lora_tanh_bias_kernel(tc, x, w, a, bb, b, out):
         bb_bf = sb("bb_bf", [P, P, PACK], BF16)
         bb_codes = sb("bb_codes", [P, P], U32)
         bb_scales = sb("bb_scales", [P, P], U8)
-        bias = sb("bias", [P, TILES, 1], F32)
+        bias_rows = sb("bias_rows", [P, P], F32)
+        bias = sb("bias", [P, P], F32)
         warm = sb("warm", [P, 8], F32)
         warm_out = sb("warm_out", [P, 8], F32)
         tcs = [(t, c) for t in range(TILES) for c in range(PASSES)]
-        x_raw = [sb("x_raw%d" % c, [P, PACK, N], F32) for c in range(PASSES)]
+        x_raw = {}
         x_bf = [sb("x_bf%d" % c, [P, N, PACK], BF16) for c in range(PASSES)]
         x_codes = [sb("x_codes%d" % c, [P, N], U32) for c in range(PASSES)]
         x_scales = [sb("x_scales%d" % c, [P, N], U8) for c in range(PASSES)]
@@ -78,7 +80,7 @@ def tile_rows_lora_tanh_bias_kernel(tc, x, w, a, bb, b, out):
                 nc.scalar.copy(out=out_ap, in_=in_ap)
 
         def weave(eng, dst, src):
-            copy(eng, dst.rearrange("p (c i) j -> p c j i", i=4), src.rearrange("p j (c i) -> p c j i", i=4))
+            copy(eng, dst.rearrange("p (c i) j -> p c j i", i=RUN), src.rearrange("p j (c i) -> p c j i", i=RUN))
 
         def quantize(codes, scales, src):
             nc.vector.quantize_mx(out=codes.bitcast(FP8X4), scales=scales, in_=src.rearrange("p n j -> p (n j)"))
@@ -86,16 +88,22 @@ def tile_rows_lora_tanh_bias_kernel(tc, x, w, a, bb, b, out):
         def La():
             nc.sync.dma_start(out=a_raw[:].rearrange("p c j r -> p c (j r)"), in_=a.rearrange("(c p j) r -> p c (j r)", c=PASSES, j=PACK))
 
-        def Lx(c):
-            nc.sync.dma_start(out=x_raw[c][:], in_=x[k_rows(c), :].rearrange("(p j) n -> p j n", j=PACK))
+        def Lx(c, lo, hi):
+            raw = sb("x_raw%d%d" % (c, lo), [P, PACK, (hi - lo) * CHUNK], F32)
+            nc.sync.dma_start(out=raw[:], in_=x[k_rows(c), cols(lo, hi)].rearrange("(p j) n -> p j n", j=PACK))
+            for i in range(lo, hi):
+                x_raw[i, c] = raw[:, :, cols(i - lo, i - lo + 1)]
 
         def Lb(t):
             nc.sync.dma_start(out=bb_raw[QUAD * t:QUAD * (t + 1), :, :],
                               in_=bb[:, t * P:(t + 1) * P].rearrange("(p j) m -> p j m", j=PACK))
 
         def Lbias():
-            with nc.allow_non_contiguous_dma(reason="one bias a partition"):
-                nc.sync.dma_start(out=bias[:], in_=b.rearrange("(t p) o -> p t o", p=P))
+            nc.sync.dma_start(out=bias_rows[0:P:QUAD, :].rearrange("q (t i) -> q t i", i=QUAD),
+                              in_=b.rearrange("(t q i) o -> q t (i o)", t=TILES, i=QUAD))
+
+        def tb():
+            nc.vector.transpose(out=bias[:], in_=bias_rows[:])
 
         def Lw(c, lo, hi):
             raw = sb("w_raw%d%d" % (c, lo), [P, PACK, (hi - lo) * P], F32)
@@ -119,7 +127,7 @@ def tile_rows_lora_tanh_bias_kernel(tc, x, w, a, bb, b, out):
                 in_=a_scales[:].bitcast(I32).rearrange("p (g i) -> p g i", i=QUAD // 4).unsqueeze(2).to_broadcast([P, PASSES * PACK, TILES, QUAD // 4]))
 
         def ix(eng, c, i):
-            weave(eng, x_bf[c][:, cols(i, i + 1), :], x_raw[c][:, :, cols(i, i + 1)])
+            weave(eng, x_bf[c][:, cols(i, i + 1), :], x_raw[i, c])
 
         def qx(c, lo, hi):
             quantize(x_codes[c][:, cols(lo, hi)], x_scales[c][:, cols(lo, hi)], x_bf[c][:, cols(lo, hi), :])
@@ -148,7 +156,9 @@ def tile_rows_lora_tanh_bias_kernel(tc, x, w, a, bb, b, out):
         def wu(count):
             scratch = whole_psum.tile([P, PACK, CHUNK], F32, name="scratch", tag="whole")
             for r in range(count):
-                z_pass(scratch[:, r % PACK, :], r % PACK, 0, 0, True, True)
+                codes = a4_codes[:, 0, :, :].rearrange("p q i -> p (q i)").bitcast(FP8X4)
+                nc.tensor.matmul_mx(out=scratch[:, r % PACK, :], lhsT=codes, lhsT_scale=a4_scales[:, 0:P],
+                                    rhs=codes, rhs_scale=a4_scales[:, 0:P], start=True, stop=True)
 
         def mz(i):
             z_bank[i] = whole_psum.tile([P, PACK, CHUNK], F32, name="z_bank%d" % i, tag="whole")
@@ -189,7 +199,7 @@ def tile_rows_lora_tanh_bias_kernel(tc, x, w, a, bb, b, out):
                                     op=mybir.AluOpType.add)
 
         def th(t, lo, hi):
-            nc.scalar.activation(out=res[t][:, cols(lo, hi)], in_=pre[t][:, cols(lo, hi)], func=ACT.Tanh, bias=bias[:, t, :])
+            nc.scalar.activation(out=res[t][:, cols(lo, hi)], in_=pre[t][:, cols(lo, hi)], func=ACT.Tanh, bias=bias[:, QUAD * t:QUAD * t + 1])
 
         def St(t, lo, hi):
             nc.sync.dma_start(out=out[t * P:(t + 1) * P, cols(lo, hi)], in_=res[t][:, cols(lo, hi)])
@@ -198,98 +208,119 @@ def tile_rows_lora_tanh_bias_kernel(tc, x, w, a, bb, b, out):
             nc.scalar.activation(out=warm_out[:], in_=warm[:], func=ACT.Tanh)
 
         nc.gpsimd.memset(warm[:], 0.0)
+        nc.gpsimd.memset(bias_rows[:], 0.0)
         nc.gpsimd.memset(a_scales[:].bitcast(I32), 0)
         La()
         tbl()
-        Lx(0)
-        Lx(1)
+        Lx(0, 0, 2)
+        Lx(1, 0, 2)
+        Lbias()
         Lb(0)
         Lb(2)
         Lb(1)
         Lb(3)
-        Lw(0, 0, 2)
-        Lw(1, 0, 2)
+        Lx(0, 2, 4)
         ia("v", 0)
         ia("s", 1)
         qa()
-        ca()
+        Lx(1, 2, 4)
+        ix("s", 0, 0)
         cs()
-        Lw(0, 2, 4)
-        ix("v", 0, 0)
-        ix("s", 0, 2)
-        ix("v", 0, 1)
-        ix("s", 0, 3)
-        qx(0, 0, 2)
-        qx(0, 2, 4)
-        wu(14)
-        Lw(1, 2, 4)
+        ca()
+        ix("s", 0, 1)
+        Lw(0, 0, 1)
         ix("v", 1, 0)
-        ix("s", 1, 2)
-        Lbias()
+        wu(8)
+        Lw(1, 0, 1)
+        Lw(0, 1, 2)
         ix("v", 1, 1)
-        ix("s", 1, 3)
+        Lw(1, 1, 2)
+        qx(0, 0, 2)
+        Lw(0, 2, 3)
         qx(1, 0, 1)
+        Lw(1, 2, 3)
         qx(1, 1, 2)
-        qx(1, 2, 3)
+        ib("v")
         mz(0)
-        ib("s")
-        qx(1, 3, 4)
-        mz(1)
-        ez("s", 0)
+        tb()
         qb()
-        mz(2)
-        iw("v", 0, 0)
+        Lw(0, 3, 4)
+        ix("v", 0, 2)
+        mz(1)
+        ix("v", 0, 3)
+        ez("s", 0)
+        qx(0, 2, 4)
         ez("s", 1)
+        Lw(1, 3, 4)
         qz(0)
-        mz(3)
-        iw("v", 1, 0)
-        ez("s", 2)
-        qw(0, 0)
-        qz(1)
+        ix("v", 1, 2)
+        ix("s", 1, 3)
         ml(0)
-        qw(1, 0)
-        ez("s", 3)
+        qz(1)
+        iw("v", 0, 0)
         ml(1)
-        iw("v", 0, 1)
-        qz(2)
-        iw("v", 1, 1)
-        ml(2)
-        qz(3)
+        qx(1, 2, 3)
+        qx(1, 3, 4)
+        iw("s", 0, 1)
+        qw(0, 0)
+        mz(2)
+        el("v", 2, 0, 2)
+        iw("v", 1, 0)
+        el("s", 3, 0, 2)
+        mz(3)
+        el("s", 1, 0, 2)
         qw(0, 1)
-        qw(1, 1)
-        ml(3)
+        iw("v", 1, 1)
+        el("s", 0, 0, 2)
+        my(0, 0, 2)
+        ez("s", 2)
+        qw(1, 0)
         iw("v", 2, 0)
-        my(0, 0, 4)
+        ez("s", 3)
+        qw(1, 1)
+        qz(2)
+        ad(0, 0, 2)
+        my(1, 0, 2)
+        iw("s", 2, 1)
+        qz(3)
+        ml(2)
+        ad(1, 0, 2)
+        ml(3)
+        th(0, 0, 2)
         iw("v", 3, 0)
-        el("s", 0, 0, 4)
-        qw(2, 0)
-        my(1, 0, 4)
-        qw(3, 0)
-        el("s", 1, 0, 4)
-        ad(0, 0, 4)
-        el("s", 2, 0, 4)
-        iw("v", 2, 1)
-        iw("v", 3, 1)
-        th(0, 0, 4)
+        my(0, 2, 4)
+        th(1, 0, 2)
         qw(2, 1)
-        ad(1, 0, 4)
-        el("s", 3, 0, 4)
+        St(0, 0, 2)
+        my(1, 2, 4)
+        qw(2, 0)
+        el("s", 0, 2, 4)
+        qw(3, 0)
+        St(1, 0, 2)
+        iw("v", 3, 1)
+        el("s", 1, 2, 4)
         my(2, 0, 2)
-        St(0, 0, 4)
+        ad(0, 2, 4)
+        el("s", 2, 2, 4)
         my(2, 2, 4)
         qw(3, 1)
-        ad(2, 0, 2)
-        th(1, 0, 4)
+        el("s", 3, 2, 4)
+        ad(1, 2, 4)
+        th(0, 2, 4)
         my(3, 0, 2)
-        ad(2, 2, 4)
+        ad(2, 0, 2)
+        th(1, 2, 4)
         my(3, 2, 4)
+        ad(2, 2, 4)
+        St(0, 2, 4)
         th(2, 0, 2)
         ad(3, 0, 2)
-        St(1, 0, 4)
+        St(1, 2, 4)
         th(2, 2, 4)
         ad(3, 2, 4)
+        St(2, 0, 2)
         th(3, 0, 2)
-        St(2, 0, 4)
+        St(2, 2, 4)
         th(3, 2, 4)
         St(3, 0, 2)
         St(3, 2, 4)

@@ -230,7 +230,6 @@ def tile_rows_lora_tanh_bias_kernel(tc, x, w, a, bb, b, out):
         ix("s", 0, 1)
         Lw(0, 0, 1)
         ix("v", 1, 0)
-        wu(8)
         Lw(1, 0, 1)
         Lw(0, 1, 2)
         ix("v", 1, 1)

@@ -17,10 +17,15 @@ P = 128
 PACK = 4
 PASSES = K // (P * PACK)
 QUAD = 32
+QUADS = P // QUAD
 TILES = M // P
 CHUNK = 128
 RUN = 2
 CHUNKS = N // CHUNK
+HALVES = 2
+SIDE = P // 2
+WIDE = PACK * P + SIDE
+BBW = P + P // 4
 
 
 def tile_rows_lora_tanh_bias_kernel(tc, x, w, a, bb, b, out):
@@ -40,36 +45,34 @@ def tile_rows_lora_tanh_bias_kernel(tc, x, w, a, bb, b, out):
         def cols(lo, hi):
             return slice(lo * CHUNK, hi * CHUNK)
 
-        a_raw = sb("a_raw", [P, PASSES, PACK, R], F32)
-        a_bf = sb("a_bf", [P, PASSES, PACK, QUAD, PACK], BF16)
-        a_codes = sb("a_codes", [P, PASSES * PACK, QUAD], U32)
-        a_scales = sb("a_scales", [P, PASSES * R], U8)
-        a4_codes = sb("a4_codes", [P, PASSES * PACK, TILES, QUAD], U32)
-        a4_scales = sb("a4_scales", [P, PASSES * PACK * P], U8)
+        a_raw = [sb("a_raw%d" % c, [P, PACK, R], F32) for c in range(PASSES)]
+        a_bf = [sb("a_bf%d" % c, [P, PACK, QUAD, PACK], BF16) for c in range(PASSES)]
+        a_codes = [sb("a_codes%d" % c, [P, PACK, QUAD], U32) for c in range(PASSES)]
+        a_scales = [sb("a_scales%d" % c, [P, PACK * QUAD], U8) for c in range(PASSES)]
+        a2_codes = [sb("a2_codes%d" % c, [P, WIDE], U32) for c in range(PASSES)]
+        a2_scales = [sb("a2_scales%d" % c, [P, WIDE], U8) for c in range(PASSES)]
         bb_raw = sb("bb_raw", [P, PACK, P], F32)
         bb_bf = sb("bb_bf", [P, P, PACK], BF16)
-        bb_codes = sb("bb_codes", [P, P], U32)
-        bb_scales = sb("bb_scales", [P, P], U8)
-        bias_rows = sb("bias_rows", [P, P], F32)
-        bias = sb("bias", [P, P], F32)
-        warm = sb("warm", [P, 8], F32)
-        warm_out = sb("warm_out", [P, 8], F32)
+        bb_own = sb("bb_own", [P, BBW], U32)
+        bb_far = sb("bb_far", [P, BBW], U32)
+        bias_rows = sb("bias_rows", [P, QUAD], F32)
+        bias = sb("bias", [P, QUAD], F32)
         tcs = [(t, c) for t in range(TILES) for c in range(PASSES)]
         x_raw = {}
         x_bf = [sb("x_bf%d" % c, [P, N, PACK], BF16) for c in range(PASSES)]
         x_codes = [sb("x_codes%d" % c, [P, N], U32) for c in range(PASSES)]
         x_scales = [sb("x_scales%d" % c, [P, N], U8) for c in range(PASSES)]
         w_raw = {}
-        w_bf = {k: sb("w_bf%d%d" % k, [P, P, PACK], BF16) for k in tcs}
-        w_codes = {k: sb("w_codes%d%d" % k, [P, P], U32) for k in tcs}
-        w_scales = {k: sb("w_scales%d%d" % k, [P, P], U8) for k in tcs}
-        z_bf = [sb("z_bf%d" % i, [P, CHUNK, PACK], BF16) for i in range(CHUNKS)]
-        z_codes = [sb("z_codes%d" % i, [P, CHUNK], U32) for i in range(CHUNKS)]
-        z_scales = [sb("z_scales%d" % i, [P, CHUNK], U8) for i in range(CHUNKS)]
-        low = [sb("low%d" % t, [P, N], F32) for t in range(TILES)]
+        w_bf = [sb("w_bf%d" % t, [P, PASSES, P, PACK], BF16) for t in range(TILES)]
+        w_codes = [sb("w_codes%d" % t, [P, PASSES * P], U32) for t in range(TILES)]
+        w_scales = [sb("w_scales%d" % t, [P, PASSES * P], U8) for t in range(TILES)]
+        z_bf = [sb("z_bf%d" % h, [P, CHUNK, PACK], BF16) for h in range(HALVES)]
+        z_codes = [sb("z_codes%d" % h, [P, CHUNK], U32) for h in range(HALVES)]
+        z_scales = [sb("z_scales%d" % h, [P, CHUNK], U8) for h in range(HALVES)]
+        low = [sb("low%d" % par, [P, CHUNKS, 2, CHUNK], F32) for par in range(2)]
         pre = [sb("pre%d" % t, [P, N], F32) for t in range(TILES)]
         res = [sb("res%d" % t, [P, N], F32) for t in range(TILES)]
-        low_bank = [row_psum.tile([P, N], F32, name="low_bank%d" % t) for t in range(TILES)]
+        low_bank = [row_psum.tile([P, N], F32, name="low_bank%d" % q) for q in range(QUADS)]
         z_bank = {}
         y_bank = {}
 
@@ -85,21 +88,27 @@ def tile_rows_lora_tanh_bias_kernel(tc, x, w, a, bb, b, out):
         def quantize(codes, scales, src):
             nc.vector.quantize_mx(out=codes.bitcast(FP8X4), scales=scales, in_=src.rearrange("p n j -> p (n j)"))
 
-        def La():
-            nc.sync.dma_start(out=a_raw[:].rearrange("p c j r -> p c (j r)"), in_=a.rearrange("(c p j) r -> p c (j r)", c=PASSES, j=PACK))
+        def La(c):
+            nc.sync.dma_start(out=a_raw[c][:], in_=a[k_rows(c), :].rearrange("(p j) r -> p j r", j=PACK))
 
-        def Lx(c, lo, hi):
+        def Lxs(c, lo, hi):
             raw = sb("x_raw%d%d" % (c, lo), [P, PACK, (hi - lo) * CHUNK], F32)
             nc.sync.dma_start(out=raw[:], in_=x[k_rows(c), cols(lo, hi)].rearrange("(p j) n -> p j n", j=PACK))
             for i in range(lo, hi):
-                x_raw[i, c] = raw[:, :, cols(i - lo, i - lo + 1)]
+                x_raw[c, i] = (raw, lo)
+
+        def Lx(c, h):
+            Lxs(c, 2 * h, 2 * h + 2)
+
+        def Lxq(c, i):
+            Lxs(c, i, i + 1)
 
         def Lb(t):
             nc.sync.dma_start(out=bb_raw[QUAD * t:QUAD * (t + 1), :, :],
                               in_=bb[:, t * P:(t + 1) * P].rearrange("(p j) m -> p j m", j=PACK))
 
         def Lbias():
-            nc.sync.dma_start(out=bias_rows[0:P:QUAD, :].rearrange("q (t i) -> q t i", i=QUAD),
+            nc.sync.dma_start(out=bias_rows[0:P:8, :],
                               in_=b.rearrange("(t q i) o -> q t (i o)", t=TILES, i=QUAD))
 
         def tb():
@@ -112,22 +121,25 @@ def tile_rows_lora_tanh_bias_kernel(tc, x, w, a, bb, b, out):
                 w_raw[t, c] = raw[:, :, (t - lo) * P:(t - lo + 1) * P]
 
         def ia(eng, c):
-            copy(eng, a_bf[:, c, :, :, :], a_raw[:, c, :, :].rearrange("p j (i s) -> p s i j", s=PACK))
+            copy(eng, a_bf[c][:].rearrange("p s i j -> p i s j"), a_raw[c][:].rearrange("p j (i s) -> p i s j", s=PACK))
 
-        def qa():
-            quantize(a_codes[:].rearrange("p g i -> p (g i)"), a_scales[:], a_bf[:].rearrange("p c s i j -> p (c s i) j"))
+        def qa(c):
+            quantize(a_codes[c][:].rearrange("p g i -> p (g i)"), a_scales[c][:], a_bf[c][:].rearrange("p s i j -> p (s i) j"))
 
-        def ca():
-            nc.vector.tensor_copy(out=a4_codes[:].bitcast(I32),
-                                  in_=a_codes[:].bitcast(I32).unsqueeze(2).to_broadcast([P, PASSES * PACK, TILES, QUAD]))
+        def ca(c):
+            dst = a2_codes[c][:, 0:PACK * P].bitcast(I32).rearrange("p (g q i) -> p g q i", q=QUADS, i=QUAD)
+            nc.vector.tensor_copy(out=dst[:, :, 2:4, :],
+                                  in_=a_codes[c][:].bitcast(I32).unsqueeze(2).to_broadcast([P, PACK, 2, QUAD]))
 
-        def cs():
+        def cs(c):
+            dst = a2_scales[c][:, 0:PACK * P].bitcast(I32).rearrange("p (g q i) -> p g q i", q=QUADS, i=QUAD // 4)
             nc.vector.tensor_copy(
-                out=a4_scales[:].bitcast(I32).rearrange("p (g q i) -> p g q i", q=TILES, i=QUAD // 4),
-                in_=a_scales[:].bitcast(I32).rearrange("p (g i) -> p g i", i=QUAD // 4).unsqueeze(2).to_broadcast([P, PASSES * PACK, TILES, QUAD // 4]))
+                out=dst[:, :, 2:4, :],
+                in_=a_scales[c][:].bitcast(I32).rearrange("p (g i) -> p g i", i=QUAD // 4).unsqueeze(2).to_broadcast([P, PACK, 2, QUAD // 4]))
 
-        def ix(eng, c, i):
-            weave(eng, x_bf[c][:, cols(i, i + 1), :], x_raw[i, c])
+        def ix(eng, c, lo, hi):
+            raw, at = x_raw[c, lo]
+            weave(eng, x_bf[c][:, cols(lo, hi), :], raw[:, :, cols(lo - at, hi - at)])
 
         def qx(c, lo, hi):
             quantize(x_codes[c][:, cols(lo, hi)], x_scales[c][:, cols(lo, hi)], x_bf[c][:, cols(lo, hi), :])
@@ -136,190 +148,197 @@ def tile_rows_lora_tanh_bias_kernel(tc, x, w, a, bb, b, out):
             weave(eng, bb_bf[:], bb_raw[:])
 
         def qb():
-            quantize(bb_codes[:], bb_scales[:], bb_bf[:])
+            quantize(bb_own[:, 0:P], bb_own[:, P:BBW].bitcast(U8), bb_bf[:])
+
+        def swap():
+            nc.sync.dma_start(out=bb_far[0:SIDE, :].bitcast(I32), in_=bb_own[SIDE:P, :].bitcast(I32))
+            nc.sync.dma_start(out=bb_far[SIDE:P, :].bitcast(I32), in_=bb_own[0:SIDE, :].bitcast(I32))
 
         def iw(eng, t, c):
-            weave(eng, w_bf[t, c][:], w_raw[t, c])
+            weave(eng, w_bf[t][:, c, :, :], w_raw[t, c])
 
-        def qw(t, c):
-            quantize(w_codes[t, c][:], w_scales[t, c][:], w_bf[t, c][:])
+        def qw(t, lo, hi):
+            quantize(w_codes[t][:, lo * P:hi * P], w_scales[t][:, lo * P:hi * P],
+                     w_bf[t][:, lo:hi, :, :].rearrange("p c m j -> p (c m) j"))
 
-        def z_pass(dst, s, i, c, start, stop):
-            g = c * PACK + s
-            nc.tensor.matmul_mx(
-                out=dst,
-                lhsT=a4_codes[:, g, :, :].rearrange("p q i -> p (q i)").bitcast(FP8X4),
-                lhsT_scale=a4_scales[:, g * P:(g + 1) * P],
-                rhs=x_codes[c][:, cols(i, i + 1)].bitcast(FP8X4), rhs_scale=x_scales[c][:, cols(i, i + 1)],
-                start=start, stop=stop)
-
-        def wu(count):
-            scratch = whole_psum.tile([P, PACK, CHUNK], F32, name="scratch", tag="whole")
-            for r in range(count):
-                codes = a4_codes[:, 0, :, :].rearrange("p q i -> p (q i)").bitcast(FP8X4)
-                nc.tensor.matmul_mx(out=scratch[:, r % PACK, :], lhsT=codes, lhsT_scale=a4_scales[:, 0:P],
-                                    rhs=codes, rhs_scale=a4_scales[:, 0:P], start=True, stop=True)
-
-        def mz(i):
-            z_bank[i] = whole_psum.tile([P, PACK, CHUNK], F32, name="z_bank%d" % i, tag="whole")
+        def mz(h, c, j):
+            if c == 0 and j == 0:
+                z_bank[h] = whole_psum.tile([P, PACK, CHUNK], F32, name="z_bank%d" % h, tag="whole")
+            i = 2 * h + j
             for s in range(PACK):
-                for c in range(PASSES):
-                    z_pass(z_bank[i][:, s, :], s, i, c, c == 0, c == PASSES - 1)
-
-        def ez(eng, i):
-            copy(eng, z_bf[i][:], z_bank[i][:].rearrange("p s n -> p n s"))
-
-        def qz(i):
-            quantize(z_codes[i][:], z_scales[i][:], z_bf[i][:])
-
-        def ml(i):
-            for t in range(TILES):
-                rows = slice(QUAD * t, QUAD * (t + 1))
+                at = s * P + (1 - j) * SIDE
                 nc.tensor.matmul_mx(
-                    out=low_bank[t][:, cols(i, i + 1)],
-                    lhsT=bb_codes[rows, :].bitcast(FP8X4), lhsT_scale=bb_scales[rows, :],
-                    rhs=z_codes[i][rows, :].bitcast(FP8X4), rhs_scale=z_scales[i][rows, :],
-                    start=True, stop=True)
+                    out=z_bank[h][:, s, :],
+                    lhsT=a2_codes[c][:, at:at + P].bitcast(FP8X4), lhsT_scale=a2_scales[c][:, at:at + P],
+                    rhs=x_codes[c][:, cols(i, i + 1)].bitcast(FP8X4), rhs_scale=x_scales[c][:, cols(i, i + 1)],
+                    start=(c == 0 and j == 0 and s == 0), stop=(c == PASSES - 1 and j == 1 and s == PACK - 1))
 
-        def el(eng, t, lo, hi):
-            copy(eng, low[t][:, cols(lo, hi)], low_bank[t][:, cols(lo, hi)])
+        def ez(eng, h):
+            copy(eng, z_bf[h][:], z_bank[h][:].rearrange("p s n -> p n s"))
 
-        def my(t, lo, hi):
-            y_bank[t, lo] = whole_psum.tile([P, (hi - lo) * CHUNK], F32, name="y_bank%d%d" % (t, lo), tag="whole")
-            for i in range(lo, hi):
-                for c in range(PASSES):
+        def qz(h):
+            quantize(z_codes[h][:], z_scales[h][:], z_bf[h][:])
+
+        def ml(h, par):
+            for u in range(2):
+                for side in range(2):
+                    q = par + 2 * side
+                    rows = slice(QUAD * q, QUAD * (q + 1))
+                    src = bb_own if q // 2 == u else bb_far
                     nc.tensor.matmul_mx(
-                        out=y_bank[t, lo][:, cols(i - lo, i - lo + 1)],
-                        lhsT=w_codes[t, c][:].bitcast(FP8X4), lhsT_scale=w_scales[t, c][:],
-                        rhs=x_codes[c][:, cols(i, i + 1)].bitcast(FP8X4), rhs_scale=x_scales[c][:, cols(i, i + 1)],
-                        start=(c == 0), stop=(c == PASSES - 1))
+                        out=low_bank[q][:, cols(2 * h + u, 2 * h + u + 1)],
+                        lhsT=src[rows, 0:P].bitcast(FP8X4), lhsT_scale=src[rows, P:BBW].bitcast(U8),
+                        rhs=z_codes[h][rows, :].bitcast(FP8X4), rhs_scale=z_scales[h][rows, :],
+                        start=True, stop=True)
 
-        def ad(t, lo, hi):
-            nc.vector.tensor_tensor(out=pre[t][:, cols(lo, hi)], in0=y_bank[t, lo][:], in1=low[t][:, cols(lo, hi)],
-                                    op=mybir.AluOpType.add)
+        def el(eng, q, h):
+            copy(eng, low[q % 2][:, 2 * h + q // 2, :, :].rearrange("p u n -> p (u n)"), low_bank[q][:, cols(2 * h, 2 * h + 2)])
+
+        def my(t, c, lo, hi):
+            if c == 0:
+                y_bank[t, lo] = whole_psum.tile([P, (hi - lo) * CHUNK], F32, name="y_bank%d%d" % (t, lo), tag="whole")
+            for i in range(lo, hi):
+                nc.tensor.matmul_mx(
+                    out=y_bank[t, lo][:, cols(i - lo, i - lo + 1)],
+                    lhsT=w_codes[t][:, c * P:(c + 1) * P].bitcast(FP8X4), lhsT_scale=w_scales[t][:, c * P:(c + 1) * P],
+                    rhs=x_codes[c][:, cols(i, i + 1)].bitcast(FP8X4), rhs_scale=x_scales[c][:, cols(i, i + 1)],
+                    start=(c == 0 and i == lo), stop=(c == PASSES - 1 and i == hi - 1))
+
+        def ad(t, lo, hi, at=None):
+            at = lo if at is None else at
+            nc.vector.tensor_tensor(out=pre[t][:, cols(lo, hi)].rearrange("p (i n) -> p i n", n=CHUNK),
+                                    in0=y_bank[t, at][:, cols(lo - at, hi - at)].rearrange("p (i n) -> p i n", n=CHUNK),
+                                    in1=low[t % 2][:, lo:hi, t // 2, :], op=mybir.AluOpType.add)
 
         def th(t, lo, hi):
-            nc.scalar.activation(out=res[t][:, cols(lo, hi)], in_=pre[t][:, cols(lo, hi)], func=ACT.Tanh, bias=bias[:, QUAD * t:QUAD * t + 1])
+            nc.scalar.activation(out=res[t][:, cols(lo, hi)], in_=pre[t][:, cols(lo, hi)], func=ACT.Tanh, bias=bias[:, 8 * t:8 * t + 1])
 
         def St(t, lo, hi):
             nc.sync.dma_start(out=out[t * P:(t + 1) * P, cols(lo, hi)], in_=res[t][:, cols(lo, hi)])
 
-        def tbl():
-            nc.scalar.activation(out=warm_out[:], in_=warm[:], func=ACT.Tanh)
-
-        nc.gpsimd.memset(warm[:], 0.0)
+        nc.gpsimd.memset(bb_own[:, P:BBW].bitcast(I32), 0)
+        for c in range(PASSES):
+            nc.gpsimd.memset(a_scales[c][:].bitcast(I32), 0)
         nc.gpsimd.memset(bias_rows[:], 0.0)
-        nc.gpsimd.memset(a_scales[:].bitcast(I32), 0)
-        La()
-        tbl()
-        Lx(0, 0, 2)
-        Lx(1, 0, 2)
-        Lbias()
+        for c in range(PASSES):
+            nc.vector.memset(a2_codes[c][:].bitcast(I32), 0)
+            nc.vector.memset(a2_scales[c][:].bitcast(I32), 0)
+        La(0)
+        Lx(0,0)
+        La(1)
         Lb(0)
         Lb(2)
         Lb(1)
         Lb(3)
-        Lx(0, 2, 4)
-        ia("v", 0)
-        ia("s", 1)
-        qa()
-        Lx(1, 2, 4)
-        ix("s", 0, 0)
-        cs()
-        ca()
-        ix("s", 0, 1)
-        Lw(0, 0, 1)
-        ix("v", 1, 0)
-        Lw(1, 0, 1)
-        Lw(0, 1, 2)
-        ix("v", 1, 1)
-        Lw(1, 1, 2)
-        qx(0, 0, 2)
-        Lw(0, 2, 3)
-        qx(1, 0, 1)
-        Lw(1, 2, 3)
-        qx(1, 1, 2)
+        Lxq(1,0)
+        Lxq(1,1)
+        Lx(0,1)
+        Lbias()
+        ia("s",0)
+        qa(0)
+        ix("s",0,1,2)
+        ix("v",0,0,1)
+        ca(0)
+        cs(0)
+        ia("s",1)
+        qx(0,0,2)
+        mz(0,0,0)
+        mz(0,0,1)
         ib("v")
-        mz(0)
-        tb()
+        qa(1)
         qb()
-        Lw(0, 3, 4)
-        ix("v", 0, 2)
-        mz(1)
-        ix("v", 0, 3)
-        ez("s", 0)
-        qx(0, 2, 4)
-        ez("s", 1)
-        Lw(1, 3, 4)
+        Lxq(1,2)
+        swap()
+        Lxq(1,3)
+        Lw(0,0,1)
+        Lw(1,0,1)
+        Lw(0,1,2)
+        Lw(1,1,2)
+        Lw(0,2,3)
+        Lw(1,2,3)
+        Lw(0,3,4)
+        Lw(1,3,4)
+        ix("s",1,0,1)
+        ca(1)
+        cs(1)
+        ix("v",1,1,2)
+        qx(1,0,1)
+        mz(0,1,0)
+        qx(1,1,2)
+        mz(0,1,1)
+        ix("v",0,2,3)
+        ix("s",0,3,4)
+        tb()
+        qx(0,2,3)
+        mz(1,0,0)
+        ez("s",0)
+        ix("v",1,2,3)
+        qx(0,3,4)
+        mz(1,0,1)
+        qx(1,2,3)
+        mz(1,1,0)
+        ix("v",1,3,4)
         qz(0)
-        ix("v", 1, 2)
-        ix("s", 1, 3)
-        ml(0)
+        qx(1,3,4)
+        ml(0,0)
+        mz(1,1,1)
+        ml(0,1)
+        iw("s",0,0)
+        iw("v",0,1)
+        el("s",0,0)
+        ez("s",1)
+        el("s",2,0)
+        qw(0,0,2)
+        my(0,0,0,4)
+        my(0,1,0,4)
+        iw("v",1,0)
+        iw("v",1,1)
         qz(1)
-        iw("v", 0, 0)
-        ml(1)
-        qx(1, 2, 3)
-        qx(1, 3, 4)
-        iw("s", 0, 1)
-        qw(0, 0)
-        mz(2)
-        el("v", 2, 0, 2)
-        iw("v", 1, 0)
-        el("s", 3, 0, 2)
-        mz(3)
-        el("s", 1, 0, 2)
-        qw(0, 1)
-        iw("v", 1, 1)
-        el("s", 0, 0, 2)
-        my(0, 0, 2)
-        ez("s", 2)
-        qw(1, 0)
-        iw("v", 2, 0)
-        ez("s", 3)
-        qw(1, 1)
-        qz(2)
-        ad(0, 0, 2)
-        my(1, 0, 2)
-        iw("s", 2, 1)
-        qz(3)
-        ml(2)
-        ad(1, 0, 2)
-        ml(3)
-        th(0, 0, 2)
-        iw("v", 3, 0)
-        my(0, 2, 4)
-        th(1, 0, 2)
-        qw(2, 1)
-        St(0, 0, 2)
-        my(1, 2, 4)
-        qw(2, 0)
-        el("s", 0, 2, 4)
-        qw(3, 0)
-        St(1, 0, 2)
-        iw("v", 3, 1)
-        el("s", 1, 2, 4)
-        my(2, 0, 2)
-        ad(0, 2, 4)
-        el("s", 2, 2, 4)
-        my(2, 2, 4)
-        qw(3, 1)
-        el("s", 3, 2, 4)
-        ad(1, 2, 4)
-        th(0, 2, 4)
-        my(3, 0, 2)
-        ad(2, 0, 2)
-        th(1, 2, 4)
-        my(3, 2, 4)
-        ad(2, 2, 4)
-        St(0, 2, 4)
-        th(2, 0, 2)
-        ad(3, 0, 2)
-        St(1, 2, 4)
-        th(2, 2, 4)
-        ad(3, 2, 4)
-        St(2, 0, 2)
-        th(3, 0, 2)
-        St(2, 2, 4)
-        th(3, 2, 4)
-        St(3, 0, 2)
-        St(3, 2, 4)
+        ml(1,0)
+        el("s",1,0)
+        el("s",3,0)
+        qw(1,0,2)
+        ml(1,1)
+        my(1,0,0,4)
+        my(1,1,0,4)
+        iw("s",2,0)
+        ad(0,0,2,0)
+        iw("v",2,1)
+        el("s",0,1)
+        el("s",2,1)
+        iw("v",3,0)
+        qw(2,0,2)
+        my(2,0,0,4)
+        my(2,1,0,4)
+        th(0,0,2)
+        St(0,0,2)
+        ad(0,2,4,0)
+        el("s",1,1)
+        el("s",3,1)
+        iw("v",3,1)
+        qw(3,0,1)
+        my(3,0,0,2)
+        my(3,0,2,4)
+        th(0,2,4)
+        St(0,2,4)
+        ad(1,0,2,0)
+        qw(3,1,2)
+        my(3,1,0,2)
+        my(3,1,2,4)
+        th(1,0,2)
+        St(1,0,2)
+        ad(1,2,4,0)
+        th(1,2,4)
+        St(1,2,4)
+        ad(2,0,2,0)
+        th(2,0,2)
+        St(2,0,2)
+        ad(2,2,4,0)
+        th(2,2,4)
+        St(2,2,4)
+        ad(3,0,2)
+        ad(3,2,4)
+        th(3,0,2)
+        St(3,0,2)
+        th(3,2,4)
+        St(3,2,4)

@@ -103,8 +103,10 @@ def tile_rows_lora_tanh_bias_kernel(tc, x, w, a, bb, b, out):
         def Lxq(c, i):
             Lxs(c, i, i + 1)
 
-        def Lb(t):
-            nc.sync.dma_start(out=bb_raw[QUAD * t:QUAD * (t + 1), :, :],
+        def Lb(q):
+            t = 2 * (q % 2) + q // 2
+            queue = nc.sync if q < 2 else nc.scalar
+            queue.dma_start(out=bb_raw[QUAD * q:QUAD * (q + 1), :, :],
                               in_=bb[:, t * P:(t + 1) * P].rearrange("(p j) m -> p j m", j=PACK))
 
         def Lbias():
@@ -208,7 +210,7 @@ def tile_rows_lora_tanh_bias_kernel(tc, x, w, a, bb, b, out):
             at = lo if at is None else at
             nc.vector.tensor_tensor(out=pre[t][:, cols(lo, hi)].rearrange("p (i n) -> p i n", n=CHUNK),
                                     in0=y_bank[t, at][:, cols(lo - at, hi - at)].rearrange("p (i n) -> p i n", n=CHUNK),
-                                    in1=low[t % 2][:, lo:hi, t // 2, :], op=mybir.AluOpType.add)
+                                    in1=low[t // 2][:, lo:hi, t % 2, :], op=mybir.AluOpType.add)
 
         def th(t, lo, hi):
             nc.scalar.activation(out=res[t][:, cols(lo, hi)], in_=pre[t][:, cols(lo, hi)], func=ACT.Tanh, bias=bias[:, 8 * t:8 * t + 1])
@@ -223,33 +225,21 @@ def tile_rows_lora_tanh_bias_kernel(tc, x, w, a, bb, b, out):
         for c in range(PASSES):
             nc.vector.memset(a2_codes[c][:].bitcast(I32), 0)
             nc.vector.memset(a2_scales[c][:].bitcast(I32), 0)
-        La(0)
-        Lx(0,0)
-        La(1)
         Lb(0)
         Lb(2)
         Lb(1)
         Lb(3)
-        Lxq(1,0)
-        Lxq(1,1)
+        La(0)
+        Lx(0,0)
+        La(1)
+        Lx(1,0)
         Lx(0,1)
         Lbias()
-        ia("s",0)
-        qa(0)
-        ix("s",0,1,2)
-        ix("v",0,0,1)
-        ca(0)
-        cs(0)
-        ia("s",1)
-        qx(0,0,2)
-        mz(0,0,0)
-        mz(0,0,1)
         ib("v")
-        qa(1)
+        ia("v",0)
         qb()
-        Lxq(1,2)
         swap()
-        Lxq(1,3)
+        Lx(1,1)
         Lw(0,0,1)
         Lw(1,0,1)
         Lw(0,1,2)
@@ -258,10 +248,21 @@ def tile_rows_lora_tanh_bias_kernel(tc, x, w, a, bb, b, out):
         Lw(1,2,3)
         Lw(0,3,4)
         Lw(1,3,4)
-        ix("s",1,0,1)
+        qa(0)
+        ix("s",0,1,2)
+        ca(0)
+        ix("v",0,0,1)
+        cs(0)
+        qx(0,0,1)
+        mz(0,0,0)
+        ia("v",1)
+        qx(0,1,2)
+        mz(0,0,1)
+        qa(1)
+        ix("s",1,1,2)
         ca(1)
         cs(1)
-        ix("v",1,1,2)
+        ix("v",1,0,1)
         qx(1,0,1)
         mz(0,1,0)
         qx(1,1,2)
@@ -272,43 +273,46 @@ def tile_rows_lora_tanh_bias_kernel(tc, x, w, a, bb, b, out):
         qx(0,2,3)
         mz(1,0,0)
         ez("s",0)
-        ix("v",1,2,3)
         qx(0,3,4)
         mz(1,0,1)
-        qx(1,2,3)
-        mz(1,1,0)
+        ix("v",1,2,3)
         ix("v",1,3,4)
         qz(0)
-        qx(1,3,4)
         ml(0,0)
+        qx(1,2,3)
+        mz(1,1,0)
+        qx(1,3,4)
         mz(1,1,1)
         ml(0,1)
         iw("s",0,0)
-        iw("v",0,1)
         el("s",0,0)
-        ez("s",1)
         el("s",2,0)
-        qw(0,0,2)
+        ez("s",1)
+        iw("v",0,1)
+        qw(0,0,1)
         my(0,0,0,4)
-        my(0,1,0,4)
         iw("v",1,0)
-        iw("v",1,1)
-        qz(1)
-        ml(1,0)
+        qw(0,1,2)
+        my(0,1,0,4)
         el("s",1,0)
         el("s",3,0)
-        qw(1,0,2)
-        ml(1,1)
+        iw("v",1,1)
+        qw(1,0,1)
+        qz(1)
+        ml(1,0)
         my(1,0,0,4)
-        my(1,1,0,4)
+        ml(1,1)
         iw("s",2,0)
+        qw(1,1,2)
+        my(1,1,0,4)
         ad(0,0,2,0)
-        iw("v",2,1)
         el("s",0,1)
         el("s",2,1)
-        iw("v",3,0)
-        qw(2,0,2)
+        iw("v",2,1)
+        qw(2,0,1)
         my(2,0,0,4)
+        iw("v",3,0)
+        qw(2,1,2)
         my(2,1,0,4)
         th(0,0,2)
         St(0,0,2)
@@ -337,8 +341,11 @@ def tile_rows_lora_tanh_bias_kernel(tc, x, w, a, bb, b, out):
         th(2,2,4)
         St(2,2,4)
         ad(3,0,2)
-        ad(3,2,4)
         th(3,0,2)
         St(3,0,2)
-        th(3,2,4)
-        St(3,2,4)
+        ad(3,2,3,2)
+        th(3,2,3)
+        St(3,2,3)
+        ad(3,3,4,2)
+        th(3,3,4)
+        St(3,3,4)

@@ -230,13 +230,13 @@ def tile_rows_lora_tanh_bias_kernel(tc, x, w, a, bb, b, out):
         Lb(1)
         Lb(3)
         La(0)
-        Lx(0,0)
         La(1)
+        Lx(0,0)
         Lx(1,0)
         Lx(0,1)
         Lbias()
         ib("v")
-        ia("v",0)
+        ia("s",0)
         qb()
         swap()
         Lx(1,1)
@@ -248,21 +248,21 @@ def tile_rows_lora_tanh_bias_kernel(tc, x, w, a, bb, b, out):
         Lw(1,2,3)
         Lw(0,3,4)
         Lw(1,3,4)
-        qa(0)
-        ix("s",0,1,2)
-        ca(0)
-        ix("v",0,0,1)
-        cs(0)
-        qx(0,0,1)
-        mz(0,0,0)
         ia("v",1)
-        qx(0,1,2)
-        mz(0,0,1)
+        qa(0)
         qa(1)
-        ix("s",1,1,2)
+        ca(0)
+        cs(0)
         ca(1)
         cs(1)
+        ix("v",0,0,1)
+        ix("s",0,1,2)
+        qx(0,0,1)
+        mz(0,0,0)
+        qx(0,1,2)
+        mz(0,0,1)
         ix("v",1,0,1)
+        ix("s",1,1,2)
         qx(1,0,1)
         mz(0,1,0)
         qx(1,1,2)
@@ -291,46 +291,46 @@ def tile_rows_lora_tanh_bias_kernel(tc, x, w, a, bb, b, out):
         iw("v",0,1)
         qw(0,0,1)
         my(0,0,0,4)
-        iw("v",1,0)
         qw(0,1,2)
         my(0,1,0,4)
+        iw("v",1,0)
         el("s",1,0)
         el("s",3,0)
-        iw("v",1,1)
         qw(1,0,1)
+        my(1,0,0,4)
+        iw("v",1,1)
         qz(1)
         ml(1,0)
-        my(1,0,0,4)
-        ml(1,1)
-        iw("s",2,0)
+        ad(0,0,2,0)
         qw(1,1,2)
         my(1,1,0,4)
-        ad(0,0,2,0)
+        ml(1,1)
+        th(0,0,2)
+        St(0,0,2)
+        iw("v",2,0)
         el("s",0,1)
         el("s",2,1)
         iw("v",2,1)
         qw(2,0,1)
         my(2,0,0,4)
-        iw("v",3,0)
+        ad(1,0,2,0)
+        iw("s",3,0)
         qw(2,1,2)
         my(2,1,0,4)
-        th(0,0,2)
-        St(0,0,2)
         ad(0,2,4,0)
-        el("s",1,1)
-        el("s",3,1)
         iw("v",3,1)
-        qw(3,0,1)
-        my(3,0,0,2)
-        my(3,0,2,4)
-        th(0,2,4)
-        St(0,2,4)
-        ad(1,0,2,0)
-        qw(3,1,2)
-        my(3,1,0,2)
-        my(3,1,2,4)
         th(1,0,2)
         St(1,0,2)
+        el("s",1,1)
+        el("s",3,1)
+        qw(3,0,1)
+        my(3,0,0,2)
+        qw(3,1,2)
+        my(3,1,0,2)
+        my(3,0,2,4)
+        my(3,1,2,4)
+        th(0,2,4)
+        St(0,2,4)
         ad(1,2,4,0)
         th(1,2,4)
         St(1,2,4)

@@ -20,7 +20,7 @@ QUAD = 32
 QUADS = P // QUAD
 TILES = M // P
 CHUNK = 128
-RUN = 2
+RUN = 4
 CHUNKS = N // CHUNK
 HALVES = 2
 SIDE = P // 2

@@ -18,21 +18,24 @@ PACK = 4
 PASSES = K // (P * PACK)
 QUAD = 32
 QUADS = P // QUAD
+SIDE = P // 2
 TILES = M // P
 CHUNK = 128
-RUN = 4
 CHUNKS = N // CHUNK
-HALVES = 2
-SIDE = P // 2
-WIDE = PACK * P + SIDE
-BBW = P + P // 4
+HALVES = CHUNKS // 2
+RUN = 4
+A_WIDTH = PACK * P + SIDE
+BB_WORDS = P + P // 4
+BIAS_STEP = P // (TILES * QUADS)
+WHOLE_BANKS = 4
 
 
 def tile_rows_lora_tanh_bias_kernel(tc, x, w, a, bb, b, out):
     nc = tc.nc
+    vec, act = nc.vector.tensor_copy, nc.scalar.copy
     with ExitStack() as ctx:
         keep = ctx.enter_context(tc.tile_pool(name="keep", bufs=1))
-        whole_psum = ctx.enter_context(tc.psum_pool(name="whole_psum", bufs=4))
+        whole_psum = ctx.enter_context(tc.psum_pool(name="whole_psum", bufs=WHOLE_BANKS))
         row_psum = ctx.enter_context(tc.psum_pool(name="row_psum", bufs=1))
         ctx.enter_context(tc.manual_schedule())
 
@@ -49,15 +52,14 @@ def tile_rows_lora_tanh_bias_kernel(tc, x, w, a, bb, b, out):
         a_bf = [sb("a_bf%d" % c, [P, PACK, QUAD, PACK], BF16) for c in range(PASSES)]
         a_codes = [sb("a_codes%d" % c, [P, PACK, QUAD], U32) for c in range(PASSES)]
         a_scales = [sb("a_scales%d" % c, [P, PACK * QUAD], U8) for c in range(PASSES)]
-        a2_codes = [sb("a2_codes%d" % c, [P, WIDE], U32) for c in range(PASSES)]
-        a2_scales = [sb("a2_scales%d" % c, [P, WIDE], U8) for c in range(PASSES)]
+        win_codes = [sb("win_codes%d" % c, [P, A_WIDTH], U32) for c in range(PASSES)]
+        win_scales = [sb("win_scales%d" % c, [P, A_WIDTH], U8) for c in range(PASSES)]
         bb_raw = sb("bb_raw", [P, PACK, P], F32)
         bb_bf = sb("bb_bf", [P, P, PACK], BF16)
-        bb_own = sb("bb_own", [P, BBW], U32)
-        bb_far = sb("bb_far", [P, BBW], U32)
+        bb_own = sb("bb_own", [P, BB_WORDS], U32)
+        bb_far = sb("bb_far", [P, BB_WORDS], U32)
         bias_rows = sb("bias_rows", [P, QUAD], F32)
         bias = sb("bias", [P, QUAD], F32)
-        tcs = [(t, c) for t in range(TILES) for c in range(PASSES)]
         x_raw = {}
         x_bf = [sb("x_bf%d" % c, [P, N, PACK], BF16) for c in range(PASSES)]
         x_codes = [sb("x_codes%d" % c, [P, N], U32) for c in range(PASSES)]
@@ -69,134 +71,106 @@ def tile_rows_lora_tanh_bias_kernel(tc, x, w, a, bb, b, out):
         z_bf = [sb("z_bf%d" % h, [P, CHUNK, PACK], BF16) for h in range(HALVES)]
         z_codes = [sb("z_codes%d" % h, [P, CHUNK], U32) for h in range(HALVES)]
         z_scales = [sb("z_scales%d" % h, [P, CHUNK], U8) for h in range(HALVES)]
-        low = [sb("low%d" % par, [P, CHUNKS, 2, CHUNK], F32) for par in range(2)]
+        low = [sb("low%d" % pair, [P, CHUNKS, 2, CHUNK], F32) for pair in range(2)]
         pre = [sb("pre%d" % t, [P, N], F32) for t in range(TILES)]
         res = [sb("res%d" % t, [P, N], F32) for t in range(TILES)]
         low_bank = [row_psum.tile([P, N], F32, name="low_bank%d" % q) for q in range(QUADS)]
         z_bank = {}
         y_bank = {}
 
-        def copy(eng, out_ap, in_ap):
-            if eng == "v":
-                nc.vector.tensor_copy(out=out_ap, in_=in_ap)
-            else:
-                nc.scalar.copy(out=out_ap, in_=in_ap)
-
-        def weave(eng, dst, src):
-            copy(eng, dst.rearrange("p (c i) j -> p c j i", i=RUN), src.rearrange("p j (c i) -> p c j i", i=RUN))
+        def weave(copy, dst, src):
+            copy(out=dst.rearrange("p (c i) j -> p c j i", i=RUN), in_=src.rearrange("p j (c i) -> p c j i", i=RUN))
 
         def quantize(codes, scales, src):
             nc.vector.quantize_mx(out=codes.bitcast(FP8X4), scales=scales, in_=src.rearrange("p n j -> p (n j)"))
 
-        def La(c):
-            nc.sync.dma_start(out=a_raw[c][:], in_=a[k_rows(c), :].rearrange("(p j) r -> p j r", j=PACK))
-
-        def Lxs(c, lo, hi):
-            raw = sb("x_raw%d%d" % (c, lo), [P, PACK, (hi - lo) * CHUNK], F32)
-            nc.sync.dma_start(out=raw[:], in_=x[k_rows(c), cols(lo, hi)].rearrange("(p j) n -> p j n", j=PACK))
-            for i in range(lo, hi):
-                x_raw[c, i] = (raw, lo)
-
-        def Lx(c, h):
-            Lxs(c, 2 * h, 2 * h + 2)
-
-        def Lxq(c, i):
-            Lxs(c, i, i + 1)
-
-        def Lb(q):
+        def load_bb(q):
             t = 2 * (q % 2) + q // 2
             queue = nc.sync if q < 2 else nc.scalar
             queue.dma_start(out=bb_raw[QUAD * q:QUAD * (q + 1), :, :],
-                              in_=bb[:, t * P:(t + 1) * P].rearrange("(p j) m -> p j m", j=PACK))
+                            in_=bb[:, t * P:(t + 1) * P].rearrange("(p j) m -> p j m", j=PACK))
 
-        def Lbias():
-            nc.sync.dma_start(out=bias_rows[0:P:8, :],
-                              in_=b.rearrange("(t q i) o -> q t (i o)", t=TILES, i=QUAD))
+        def load_a(c):
+            nc.sync.dma_start(out=a_raw[c][:], in_=a[k_rows(c), :].rearrange("(p j) r -> p j r", j=PACK))
 
-        def tb():
+        def load_x(c, h):
+            x_raw[c, h] = sb("x_raw%d%d" % (c, h), [P, PACK, 2 * CHUNK], F32)
+            nc.sync.dma_start(out=x_raw[c, h][:], in_=x[k_rows(c), cols(2 * h, 2 * h + 2)].rearrange("(p j) n -> p j n", j=PACK))
+
+        def load_w(t, c):
+            w_raw[t, c] = sb("w_raw%d%d" % (t, c), [P, PACK, P], F32)
+            nc.sync.dma_start(out=w_raw[t, c][:], in_=w[k_rows(c), t * P:(t + 1) * P].rearrange("(p j) m -> p j m", j=PACK))
+
+        def load_bias():
+            nc.sync.dma_start(out=bias_rows[0:P:BIAS_STEP, :], in_=b.rearrange("(t q i) o -> q t (i o)", t=TILES, i=QUAD))
+
+        def turn_bias():
             nc.vector.transpose(out=bias[:], in_=bias_rows[:])
 
-        def Lw(c, lo, hi):
-            raw = sb("w_raw%d%d" % (c, lo), [P, PACK, (hi - lo) * P], F32)
-            nc.sync.dma_start(out=raw[:], in_=w[k_rows(c), lo * P:hi * P].rearrange("(p j) m -> p j m", j=PACK))
-            for t in range(lo, hi):
-                w_raw[t, c] = raw[:, :, (t - lo) * P:(t - lo + 1) * P]
+        def quantize_bb():
+            quantize(bb_own[:, 0:P], bb_own[:, P:BB_WORDS].bitcast(U8), bb_bf[:])
 
-        def ia(eng, c):
-            copy(eng, a_bf[c][:].rearrange("p s i j -> p i s j"), a_raw[c][:].rearrange("p j (i s) -> p i s j", s=PACK))
-
-        def qa(c):
-            quantize(a_codes[c][:].rearrange("p g i -> p (g i)"), a_scales[c][:], a_bf[c][:].rearrange("p s i j -> p (s i) j"))
-
-        def ca(c):
-            dst = a2_codes[c][:, 0:PACK * P].bitcast(I32).rearrange("p (g q i) -> p g q i", q=QUADS, i=QUAD)
-            nc.vector.tensor_copy(out=dst[:, :, 2:4, :],
-                                  in_=a_codes[c][:].bitcast(I32).unsqueeze(2).to_broadcast([P, PACK, 2, QUAD]))
-
-        def cs(c):
-            dst = a2_scales[c][:, 0:PACK * P].bitcast(I32).rearrange("p (g q i) -> p g q i", q=QUADS, i=QUAD // 4)
-            nc.vector.tensor_copy(
-                out=dst[:, :, 2:4, :],
-                in_=a_scales[c][:].bitcast(I32).rearrange("p (g i) -> p g i", i=QUAD // 4).unsqueeze(2).to_broadcast([P, PACK, 2, QUAD // 4]))
-
-        def ix(eng, c, lo, hi):
-            raw, at = x_raw[c, lo]
-            weave(eng, x_bf[c][:, cols(lo, hi), :], raw[:, :, cols(lo - at, hi - at)])
-
-        def qx(c, lo, hi):
-            quantize(x_codes[c][:, cols(lo, hi)], x_scales[c][:, cols(lo, hi)], x_bf[c][:, cols(lo, hi), :])
-
-        def ib(eng):
-            weave(eng, bb_bf[:], bb_raw[:])
-
-        def qb():
-            quantize(bb_own[:, 0:P], bb_own[:, P:BBW].bitcast(U8), bb_bf[:])
-
-        def swap():
+        def swap_bb():
             nc.sync.dma_start(out=bb_far[0:SIDE, :].bitcast(I32), in_=bb_own[SIDE:P, :].bitcast(I32))
             nc.sync.dma_start(out=bb_far[SIDE:P, :].bitcast(I32), in_=bb_own[0:SIDE, :].bitcast(I32))
 
-        def iw(eng, t, c):
-            weave(eng, w_bf[t][:, c, :, :], w_raw[t, c])
+        def weave_a(copy, c):
+            copy(out=a_bf[c][:].rearrange("p s d j -> p d s j"), in_=a_raw[c][:].rearrange("p j (d s) -> p d s j", s=PACK))
 
-        def qw(t, lo, hi):
-            quantize(w_codes[t][:, lo * P:hi * P], w_scales[t][:, lo * P:hi * P],
-                     w_bf[t][:, lo:hi, :, :].rearrange("p c m j -> p (c m) j"))
+        def quantize_a(c):
+            quantize(a_codes[c][:].rearrange("p s d -> p (s d)"), a_scales[c][:], a_bf[c][:].rearrange("p s d j -> p (s d) j"))
 
-        def mz(h, c, j):
-            if c == 0 and j == 0:
+        def spread_a(c):
+            for dst, src, width in ((win_codes[c], a_codes[c][:].bitcast(I32), QUAD),
+                                    (win_scales[c], a_scales[c][:].bitcast(I32).rearrange("p (s i) -> p s i", s=PACK), QUAD // 4)):
+                groups = dst[:, 0:PACK * P].bitcast(I32).rearrange("p (s q i) -> p s q i", q=QUADS, i=width)
+                nc.vector.tensor_copy(out=groups[:, :, 2:QUADS, :], in_=src.unsqueeze(2).to_broadcast([P, PACK, 2, width]))
+
+        def weave_x(copy, c, i):
+            weave(copy, x_bf[c][:, cols(i, i + 1), :], x_raw[c, i // 2][:, :, cols(i % 2, i % 2 + 1)])
+
+        def z_pass(c, i):
+            quantize(x_codes[c][:, cols(i, i + 1)], x_scales[c][:, cols(i, i + 1)], x_bf[c][:, cols(i, i + 1), :])
+            h, side = divmod(i, 2)
+            if h not in z_bank:
                 z_bank[h] = whole_psum.tile([P, PACK, CHUNK], F32, name="z_bank%d" % h, tag="whole")
-            i = 2 * h + j
             for s in range(PACK):
-                at = s * P + (1 - j) * SIDE
+                at = s * P + (1 - side) * SIDE
                 nc.tensor.matmul_mx(
                     out=z_bank[h][:, s, :],
-                    lhsT=a2_codes[c][:, at:at + P].bitcast(FP8X4), lhsT_scale=a2_scales[c][:, at:at + P],
+                    lhsT=win_codes[c][:, at:at + P].bitcast(FP8X4), lhsT_scale=win_scales[c][:, at:at + P],
                     rhs=x_codes[c][:, cols(i, i + 1)].bitcast(FP8X4), rhs_scale=x_scales[c][:, cols(i, i + 1)],
-                    start=(c == 0 and j == 0 and s == 0), stop=(c == PASSES - 1 and j == 1 and s == PACK - 1))
+                    start=(c == 0 and side == 0 and s == 0), stop=(c == PASSES - 1 and side == 1 and s == PACK - 1))
 
-        def ez(eng, h):
-            copy(eng, z_bf[h][:], z_bank[h][:].rearrange("p s n -> p n s"))
+        def round_z(h):
+            nc.scalar.copy(out=z_bf[h][:], in_=z_bank[h][:].rearrange("p s n -> p n s"))
 
-        def qz(h):
+        def quantize_z(h):
             quantize(z_codes[h][:], z_scales[h][:], z_bf[h][:])
 
-        def ml(h, par):
+        def low_products(h, pair):
             for u in range(2):
-                for side in range(2):
-                    q = par + 2 * side
+                for q in (pair, pair + 2):
                     rows = slice(QUAD * q, QUAD * (q + 1))
                     src = bb_own if q // 2 == u else bb_far
                     nc.tensor.matmul_mx(
                         out=low_bank[q][:, cols(2 * h + u, 2 * h + u + 1)],
-                        lhsT=src[rows, 0:P].bitcast(FP8X4), lhsT_scale=src[rows, P:BBW].bitcast(U8),
+                        lhsT=src[rows, 0:P].bitcast(FP8X4), lhsT_scale=src[rows, P:BB_WORDS].bitcast(U8),
                         rhs=z_codes[h][rows, :].bitcast(FP8X4), rhs_scale=z_scales[h][rows, :],
                         start=True, stop=True)
 
-        def el(eng, q, h):
-            copy(eng, low[q % 2][:, 2 * h + q // 2, :, :].rearrange("p u n -> p (u n)"), low_bank[q][:, cols(2 * h, 2 * h + 2)])
+        def copy_low(h, pair):
+            for q in (pair, pair + 2):
+                nc.scalar.copy(out=low[pair][:, 2 * h + q // 2, :, :].rearrange("p u n -> p (u n)"),
+                               in_=low_bank[q][:, cols(2 * h, 2 * h + 2)])
 
-        def my(t, c, lo, hi):
+        def weave_w(copy, t, c):
+            weave(copy, w_bf[t][:, c, :, :], w_raw[t, c][:])
+
+        def quantize_w(t, c):
+            quantize(w_codes[t][:, c * P:(c + 1) * P], w_scales[t][:, c * P:(c + 1) * P], w_bf[t][:, c, :, :])
+
+        def main_pass(t, c, lo, hi):
             if c == 0:
                 y_bank[t, lo] = whole_psum.tile([P, (hi - lo) * CHUNK], F32, name="y_bank%d%d" % (t, lo), tag="whole")
             for i in range(lo, hi):
@@ -206,146 +180,109 @@ def tile_rows_lora_tanh_bias_kernel(tc, x, w, a, bb, b, out):
                     rhs=x_codes[c][:, cols(i, i + 1)].bitcast(FP8X4), rhs_scale=x_scales[c][:, cols(i, i + 1)],
                     start=(c == 0 and i == lo), stop=(c == PASSES - 1 and i == hi - 1))
 
-        def ad(t, lo, hi, at=None):
-            at = lo if at is None else at
+        def w_pass(t, c):
+            quantize_w(t, c)
+            main_pass(t, c, 0, CHUNKS)
+
+        def add(t, lo, hi, first=0):
             nc.vector.tensor_tensor(out=pre[t][:, cols(lo, hi)].rearrange("p (i n) -> p i n", n=CHUNK),
-                                    in0=y_bank[t, at][:, cols(lo - at, hi - at)].rearrange("p (i n) -> p i n", n=CHUNK),
+                                    in0=y_bank[t, first][:, cols(lo - first, hi - first)].rearrange("p (i n) -> p i n", n=CHUNK),
                                     in1=low[t // 2][:, lo:hi, t % 2, :], op=mybir.AluOpType.add)
 
-        def th(t, lo, hi):
-            nc.scalar.activation(out=res[t][:, cols(lo, hi)], in_=pre[t][:, cols(lo, hi)], func=ACT.Tanh, bias=bias[:, 8 * t:8 * t + 1])
-
-        def St(t, lo, hi):
+        def finish(t, lo, hi):
+            nc.scalar.activation(out=res[t][:, cols(lo, hi)], in_=pre[t][:, cols(lo, hi)], func=ACT.Tanh,
+                                 bias=bias[:, BIAS_STEP * t:BIAS_STEP * t + 1])
             nc.sync.dma_start(out=out[t * P:(t + 1) * P, cols(lo, hi)], in_=res[t][:, cols(lo, hi)])
 
-        nc.gpsimd.memset(bb_own[:, P:BBW].bitcast(I32), 0)
+        nc.gpsimd.memset(bb_own[:, P:BB_WORDS].bitcast(I32), 0)
         for c in range(PASSES):
             nc.gpsimd.memset(a_scales[c][:].bitcast(I32), 0)
         nc.gpsimd.memset(bias_rows[:], 0.0)
         for c in range(PASSES):
-            nc.vector.memset(a2_codes[c][:].bitcast(I32), 0)
-            nc.vector.memset(a2_scales[c][:].bitcast(I32), 0)
-        Lb(0)
-        Lb(2)
-        Lb(1)
-        Lb(3)
-        La(0)
-        La(1)
-        Lx(0,0)
-        Lx(1,0)
-        Lx(0,1)
-        Lbias()
-        ib("v")
-        ia("s",0)
-        qb()
-        swap()
-        Lx(1,1)
-        Lw(0,0,1)
-        Lw(1,0,1)
-        Lw(0,1,2)
-        Lw(1,1,2)
-        Lw(0,2,3)
-        Lw(1,2,3)
-        Lw(0,3,4)
-        Lw(1,3,4)
-        ia("v",1)
-        qa(0)
-        qa(1)
-        ca(0)
-        cs(0)
-        ca(1)
-        cs(1)
-        ix("v",0,0,1)
-        ix("s",0,1,2)
-        qx(0,0,1)
-        mz(0,0,0)
-        qx(0,1,2)
-        mz(0,0,1)
-        ix("v",1,0,1)
-        ix("s",1,1,2)
-        qx(1,0,1)
-        mz(0,1,0)
-        qx(1,1,2)
-        mz(0,1,1)
-        ix("v",0,2,3)
-        ix("s",0,3,4)
-        tb()
-        qx(0,2,3)
-        mz(1,0,0)
-        ez("s",0)
-        qx(0,3,4)
-        mz(1,0,1)
-        ix("v",1,2,3)
-        ix("v",1,3,4)
-        qz(0)
-        ml(0,0)
-        qx(1,2,3)
-        mz(1,1,0)
-        qx(1,3,4)
-        mz(1,1,1)
-        ml(0,1)
-        iw("s",0,0)
-        el("s",0,0)
-        el("s",2,0)
-        ez("s",1)
-        iw("v",0,1)
-        qw(0,0,1)
-        my(0,0,0,4)
-        qw(0,1,2)
-        my(0,1,0,4)
-        iw("v",1,0)
-        el("s",1,0)
-        el("s",3,0)
-        qw(1,0,1)
-        my(1,0,0,4)
-        iw("v",1,1)
-        qz(1)
-        ml(1,0)
-        ad(0,0,2,0)
-        qw(1,1,2)
-        my(1,1,0,4)
-        ml(1,1)
-        th(0,0,2)
-        St(0,0,2)
-        iw("v",2,0)
-        el("s",0,1)
-        el("s",2,1)
-        iw("v",2,1)
-        qw(2,0,1)
-        my(2,0,0,4)
-        ad(1,0,2,0)
-        iw("s",3,0)
-        qw(2,1,2)
-        my(2,1,0,4)
-        ad(0,2,4,0)
-        iw("v",3,1)
-        th(1,0,2)
-        St(1,0,2)
-        el("s",1,1)
-        el("s",3,1)
-        qw(3,0,1)
-        my(3,0,0,2)
-        qw(3,1,2)
-        my(3,1,0,2)
-        my(3,0,2,4)
-        my(3,1,2,4)
-        th(0,2,4)
-        St(0,2,4)
-        ad(1,2,4,0)
-        th(1,2,4)
-        St(1,2,4)
-        ad(2,0,2,0)
-        th(2,0,2)
-        St(2,0,2)
-        ad(2,2,4,0)
-        th(2,2,4)
-        St(2,2,4)
-        ad(3,0,2)
-        th(3,0,2)
-        St(3,0,2)
-        ad(3,2,3,2)
-        th(3,2,3)
-        St(3,2,3)
-        ad(3,3,4,2)
-        th(3,3,4)
-        St(3,3,4)
+            for win, width in ((win_codes[c], SIDE), (win_scales[c], SIDE // 4)):
+                nc.vector.memset(win[:].bitcast(I32).rearrange("p (g i) -> p g i", i=width)[:, 0::2, :], 0)
+
+        for q in (0, 2, 1, 3):
+            load_bb(q)
+        for c in range(PASSES):
+            load_a(c)
+        load_x(0, 0)
+        load_x(1, 0)
+        load_x(0, 1)
+        load_bias()
+        weave(vec, bb_bf[:], bb_raw[:])
+        weave_a(act, 0)
+        quantize_bb()
+        swap_bb()
+        load_x(1, 1)
+        for t in range(TILES):
+            for c in range(PASSES):
+                load_w(t, c)
+
+        weave_a(vec, 1)
+        for c in range(PASSES):
+            quantize_a(c)
+        for c in range(PASSES):
+            spread_a(c)
+
+        for c in range(PASSES):
+            weave_x(vec, c, 0)
+            weave_x(act, c, 1)
+            z_pass(c, 0)
+            z_pass(c, 1)
+
+        weave_x(vec, 0, 2)
+        weave_x(act, 0, 3)
+        turn_bias()
+        z_pass(0, 2)
+        round_z(0)
+        z_pass(0, 3)
+        weave_x(vec, 1, 2)
+        weave_x(vec, 1, 3)
+        quantize_z(0)
+        low_products(0, 0)
+        z_pass(1, 2)
+        z_pass(1, 3)
+        low_products(0, 1)
+
+        weave_w(act, 0, 0)
+        copy_low(0, 0)
+        round_z(1)
+        weave_w(vec, 0, 1)
+        w_pass(0, 0)
+        w_pass(0, 1)
+        weave_w(vec, 1, 0)
+        copy_low(0, 1)
+        w_pass(1, 0)
+        weave_w(vec, 1, 1)
+        quantize_z(1)
+        low_products(1, 0)
+        add(0, 0, 2)
+        w_pass(1, 1)
+        low_products(1, 1)
+        finish(0, 0, 2)
+
+        weave_w(vec, 2, 0)
+        copy_low(1, 0)
+        weave_w(vec, 2, 1)
+        w_pass(2, 0)
+        add(1, 0, 2)
+        weave_w(act, 3, 0)
+        w_pass(2, 1)
+        add(0, 2, 4)
+
+        last = TILES - 1
+        weave_w(vec, last, 1)
+        finish(1, 0, 2)
+        copy_low(1, 1)
+        quantize_w(last, 0)
+        main_pass(last, 0, 0, 2)
+        quantize_w(last, 1)
+        main_pass(last, 1, 0, 2)
+        for c in range(PASSES):
+            main_pass(last, c, 2, 4)
+        finish(0, 2, 4)
+
+        for t, lo, hi, first in ((1, 2, 4, 0), (2, 0, 2, 0), (2, 2, 4, 0), (last, 0, 2, 0), (last, 2, 3, 2), (last, 3, 4, 2)):
+            add(t, lo, hi, first)
+            finish(t, lo, hi)

@@ -93,13 +93,17 @@ def tile_rows_lora_tanh_bias_kernel(tc, x, w, a, bb, b, out):
         def load_a(c):
             nc.sync.dma_start(out=a_raw[c][:], in_=a[k_rows(c), :].rearrange("(p j) r -> p j r", j=PACK))
 
-        def load_x(c, h):
-            x_raw[c, h] = sb("x_raw%d%d" % (c, h), [P, PACK, 2 * CHUNK], F32)
-            nc.sync.dma_start(out=x_raw[c, h][:], in_=x[k_rows(c), cols(2 * h, 2 * h + 2)].rearrange("(p j) n -> p j n", j=PACK))
+        def load_columns(name, src, raw, c, lo, hi):
+            both = sb("%s_raw%d%d" % (name, c, lo), [P, PACK, (hi - lo) * CHUNK], F32)
+            nc.sync.dma_start(out=both[:], in_=src[k_rows(c), cols(lo, hi)].rearrange("(p j) n -> p j n", j=PACK))
+            for i in range(lo, hi):
+                raw[c, i] = both[:, :, cols(i - lo, i - lo + 1)]
 
-        def load_w(t, c):
-            w_raw[t, c] = sb("w_raw%d%d" % (t, c), [P, PACK, P], F32)
-            nc.sync.dma_start(out=w_raw[t, c][:], in_=w[k_rows(c), t * P:(t + 1) * P].rearrange("(p j) m -> p j m", j=PACK))
+        def load_x(c, lo, hi):
+            load_columns("x", x, x_raw, c, lo, hi)
+
+        def load_w(c, lo, hi):
+            load_columns("w", w, w_raw, c, lo, hi)
 
         def load_bias():
             nc.sync.dma_start(out=bias_rows[0:P:BIAS_STEP, :], in_=b.rearrange("(t q i) o -> q t (i o)", t=TILES, i=QUAD))
@@ -127,10 +131,12 @@ def tile_rows_lora_tanh_bias_kernel(tc, x, w, a, bb, b, out):
                 nc.vector.tensor_copy(out=groups[:, :, 2:QUADS, :], in_=src.unsqueeze(2).to_broadcast([P, PACK, 2, width]))
 
         def weave_x(copy, c, i):
-            weave(copy, x_bf[c][:, cols(i, i + 1), :], x_raw[c, i // 2][:, :, cols(i % 2, i % 2 + 1)])
+            weave(copy, x_bf[c][:, cols(i, i + 1), :], x_raw[c, i])
+
+        def quantize_x(c, i):
+            quantize(x_codes[c][:, cols(i, i + 1)], x_scales[c][:, cols(i, i + 1)], x_bf[c][:, cols(i, i + 1), :])
 
         def z_pass(c, i):
-            quantize(x_codes[c][:, cols(i, i + 1)], x_scales[c][:, cols(i, i + 1)], x_bf[c][:, cols(i, i + 1), :])
             h, side = divmod(i, 2)
             if h not in z_bank:
                 z_bank[h] = whole_psum.tile([P, PACK, CHUNK], F32, name="z_bank%d" % h, tag="whole")
@@ -159,13 +165,13 @@ def tile_rows_lora_tanh_bias_kernel(tc, x, w, a, bb, b, out):
                         rhs=z_codes[h][rows, :].bitcast(FP8X4), rhs_scale=z_scales[h][rows, :],
                         start=True, stop=True)
 
-        def copy_low(h, pair):
-            for q in (pair, pair + 2):
-                nc.scalar.copy(out=low[pair][:, 2 * h + q // 2, :, :].rearrange("p u n -> p (u n)"),
-                               in_=low_bank[q][:, cols(2 * h, 2 * h + 2)])
+        def copy_low(h, pair, copies=(act, act)):
+            for q, copy in zip((pair, pair + 2), copies):
+                copy(out=low[pair][:, 2 * h + q // 2, :, :].rearrange("p u n -> p (u n)"),
+                     in_=low_bank[q][:, cols(2 * h, 2 * h + 2)])
 
         def weave_w(copy, t, c):
-            weave(copy, w_bf[t][:, c, :, :], w_raw[t, c][:])
+            weave(copy, w_bf[t][:, c, :, :], w_raw[c, t])
 
         def quantize_w(t, c):
             quantize(w_codes[t][:, c * P:(c + 1) * P], w_scales[t][:, c * P:(c + 1) * P], w_bf[t][:, c, :, :])
@@ -189,9 +195,15 @@ def tile_rows_lora_tanh_bias_kernel(tc, x, w, a, bb, b, out):
                                     in0=y_bank[t, first][:, cols(lo - first, hi - first)].rearrange("p (i n) -> p i n", n=CHUNK),
                                     in1=low[t // 2][:, lo:hi, t % 2, :], op=mybir.AluOpType.add)
 
-        def finish(t, lo, hi):
+        def tanh(t, lo, hi):
             nc.scalar.activation(out=res[t][:, cols(lo, hi)], in_=pre[t][:, cols(lo, hi)], func=ACT.Tanh,
                                  bias=bias[:, BIAS_STEP * t:BIAS_STEP * t + 1])
+
+        def finish(t, lo, hi):
+            tanh(t, lo, hi)
+            store(t, lo, hi)
+
+        def store(t, lo, hi):
             nc.sync.dma_start(out=out[t * P:(t + 1) * P, cols(lo, hi)], in_=res[t][:, cols(lo, hi)])
 
         nc.gpsimd.memset(bb_own[:, P:BB_WORDS].bitcast(I32), 0)
@@ -204,85 +216,96 @@ def tile_rows_lora_tanh_bias_kernel(tc, x, w, a, bb, b, out):
 
         for q in (0, 2, 1, 3):
             load_bb(q)
-        for c in range(PASSES):
-            load_a(c)
-        load_x(0, 0)
-        load_x(1, 0)
-        load_x(0, 1)
-        load_bias()
+        load_a(0)
+        load_x(0, 0, 4)
+        load_a(1)
+        load_x(1, 0, 2)
+        load_x(1, 2, 4)
         weave(vec, bb_bf[:], bb_raw[:])
         weave_a(act, 0)
         quantize_bb()
+        load_w(0, 0, 2)
         swap_bb()
-        load_x(1, 1)
-        for t in range(TILES):
-            for c in range(PASSES):
-                load_w(t, c)
+        load_bias()
+        load_w(1, 0, 2)
+        load_w(0, 2, 4)
+        load_w(1, 2, 3)
+        load_w(1, 3, 4)
 
-        weave_a(vec, 1)
-        for c in range(PASSES):
-            quantize_a(c)
-        for c in range(PASSES):
-            spread_a(c)
+        quantize_a(0)
+        spread_a(0)
 
-        for c in range(PASSES):
-            weave_x(vec, c, 0)
-            weave_x(act, c, 1)
-            z_pass(c, 0)
-            z_pass(c, 1)
-
-        weave_x(vec, 0, 2)
+        weave_x(vec, 0, 0)
+        weave_x(act, 0, 1)
+        weave_x(act, 0, 2)
         weave_x(act, 0, 3)
-        turn_bias()
+        quantize_x(0, 0)
+        z_pass(0, 0)
+        weave_a(vec, 1)
+        quantize_x(0, 1)
+        z_pass(0, 1)
+        quantize_a(1)
+        quantize_x(0, 2)
         z_pass(0, 2)
-        round_z(0)
+        spread_a(1)
+
+        weave_x(vec, 1, 0)
+        weave_x(act, 1, 1)
+        quantize_x(0, 3)
+        quantize_x(1, 0)
+        z_pass(1, 0)
+        quantize_x(1, 1)
+        z_pass(1, 1)
         z_pass(0, 3)
+
         weave_x(vec, 1, 2)
-        weave_x(vec, 1, 3)
+        weave_x(act, 1, 3)
+        round_z(0)
+        quantize_x(1, 2)
+        z_pass(1, 2)
+        quantize_x(1, 3)
+        z_pass(1, 3)
+        weave_w(vec, 0, 0)
+        weave_w(act, 1, 0)
         quantize_z(0)
         low_products(0, 0)
-        z_pass(1, 2)
-        z_pass(1, 3)
         low_products(0, 1)
-
-        weave_w(act, 0, 0)
-        copy_low(0, 0)
         round_z(1)
-        weave_w(vec, 0, 1)
         w_pass(0, 0)
-        w_pass(0, 1)
-        weave_w(vec, 1, 0)
-        copy_low(0, 1)
+        copy_low(0, 0)
+        turn_bias()
         w_pass(1, 0)
-        weave_w(vec, 1, 1)
         quantize_z(1)
+        copy_low(0, 1)
         low_products(1, 0)
-        add(0, 0, 2)
-        w_pass(1, 1)
         low_products(1, 1)
-        finish(0, 0, 2)
 
-        weave_w(vec, 2, 0)
+        weave_w(vec, 0, 1)
+        weave_w(vec, 1, 1)
+        w_pass(0, 1)
+        w_pass(1, 1)
         copy_low(1, 0)
-        weave_w(vec, 2, 1)
-        w_pass(2, 0)
-        add(1, 0, 2)
         weave_w(act, 3, 0)
-        w_pass(2, 1)
-        add(0, 2, 4)
 
         last = TILES - 1
-        weave_w(vec, last, 1)
-        finish(1, 0, 2)
-        copy_low(1, 1)
+        weave_w(vec, 2, 0)
+        weave_w(act, 2, 1)
+        w_pass(2, 0)
+        add(0, 0, 2)
+        finish(0, 0, 2)
         quantize_w(last, 0)
+        add(0, 2, 4)
+        finish(0, 2, 4)
+        weave_w(vec, last, 1)
+        w_pass(2, 1)
+        copy_low(1, 1)
         main_pass(last, 0, 0, 2)
+        main_pass(last, 0, 2, 4)
+        add(1, 0, 2)
         quantize_w(last, 1)
         main_pass(last, 1, 0, 2)
-        for c in range(PASSES):
-            main_pass(last, c, 2, 4)
-        finish(0, 2, 4)
-
+        main_pass(last, 1, 2, 4)
+        finish(1, 0, 2)
         for t, lo, hi, first in ((1, 2, 4, 0), (2, 0, 2, 0), (2, 2, 4, 0), (last, 0, 2, 0), (last, 2, 3, 2), (last, 3, 4, 2)):
             add(t, lo, hi, first)
             finish(t, lo, hi)

@@ -27,6 +27,7 @@ RUN = 4
 A_WIDTH = PACK * P + SIDE
 BB_WORDS = P + P // 4
 BIAS_STEP = P // (TILES * QUADS)
+SHARED = P // 2
 WHOLE_BANKS = 4
 
 
@@ -165,13 +166,15 @@ def tile_rows_lora_tanh_bias_kernel(tc, x, w, a, bb, b, out):
                         rhs=z_codes[h][rows, :].bitcast(FP8X4), rhs_scale=z_scales[h][rows, :],
                         start=True, stop=True)
 
-        def copy_low(h, pair, copies=(act, act)):
-            for q, copy in zip((pair, pair + 2), copies):
-                copy(out=low[pair][:, 2 * h + q // 2, :, :].rearrange("p u n -> p (u n)"),
-                     in_=low_bank[q][:, cols(2 * h, 2 * h + 2)])
+        def copy_bank(copy, h, q):
+            copy(out=low[q % 2][:, 2 * h + q // 2, :, :].rearrange("p u n -> p (u n)"), in_=low_bank[q][:, cols(2 * h, 2 * h + 2)])
 
-        def weave_w(copy, t, c):
-            weave(copy, w_bf[t][:, c, :, :], w_raw[c, t])
+        def copy_low(h, pair):
+            for q in (pair, pair + 2):
+                copy_bank(act, h, q)
+
+        def weave_w(copy, t, c, lo=0, hi=P):
+            weave(copy, w_bf[t][:, c, lo:hi, :], w_raw[c, t][:, :, lo:hi])
 
         def quantize_w(t, c):
             quantize(w_codes[t][:, c * P:(c + 1) * P], w_scales[t][:, c * P:(c + 1) * P], w_bf[t][:, c, :, :])
@@ -195,15 +198,9 @@ def tile_rows_lora_tanh_bias_kernel(tc, x, w, a, bb, b, out):
                                     in0=y_bank[t, first][:, cols(lo - first, hi - first)].rearrange("p (i n) -> p i n", n=CHUNK),
                                     in1=low[t // 2][:, lo:hi, t % 2, :], op=mybir.AluOpType.add)
 
-        def tanh(t, lo, hi):
+        def finish(t, lo, hi):
             nc.scalar.activation(out=res[t][:, cols(lo, hi)], in_=pre[t][:, cols(lo, hi)], func=ACT.Tanh,
                                  bias=bias[:, BIAS_STEP * t:BIAS_STEP * t + 1])
-
-        def finish(t, lo, hi):
-            tanh(t, lo, hi)
-            store(t, lo, hi)
-
-        def store(t, lo, hi):
             nc.sync.dma_start(out=out[t * P:(t + 1) * P, cols(lo, hi)], in_=res[t][:, cols(lo, hi)])
 
         nc.gpsimd.memset(bb_own[:, P:BB_WORDS].bitcast(I32), 0)
@@ -217,10 +214,10 @@ def tile_rows_lora_tanh_bias_kernel(tc, x, w, a, bb, b, out):
         for q in (0, 2, 1, 3):
             load_bb(q)
         load_a(0)
-        load_x(0, 0, 4)
+        load_x(0, 0, CHUNKS)
         load_a(1)
-        load_x(1, 0, 2)
-        load_x(1, 2, 4)
+        for h in range(HALVES):
+            load_x(1, 2 * h, 2 * h + 2)
         weave(vec, bb_bf[:], bb_raw[:])
         weave_a(act, 0)
         quantize_bb()
@@ -228,17 +225,16 @@ def tile_rows_lora_tanh_bias_kernel(tc, x, w, a, bb, b, out):
         swap_bb()
         load_bias()
         load_w(1, 0, 2)
-        load_w(0, 2, 4)
-        load_w(1, 2, 3)
-        load_w(1, 3, 4)
+        for t in range(2, TILES):
+            for c in range(PASSES):
+                load_w(c, t, t + 1)
 
         quantize_a(0)
         spread_a(0)
 
         weave_x(vec, 0, 0)
-        weave_x(act, 0, 1)
-        weave_x(act, 0, 2)
-        weave_x(act, 0, 3)
+        for i in range(1, CHUNKS):
+            weave_x(act, 0, i)
         quantize_x(0, 0)
         z_pass(0, 0)
         weave_a(vec, 1)
@@ -252,60 +248,64 @@ def tile_rows_lora_tanh_bias_kernel(tc, x, w, a, bb, b, out):
         weave_x(vec, 1, 0)
         weave_x(act, 1, 1)
         quantize_x(0, 3)
-        quantize_x(1, 0)
-        z_pass(1, 0)
-        quantize_x(1, 1)
-        z_pass(1, 1)
+        for i in (0, 1):
+            quantize_x(1, i)
+            z_pass(1, i)
         z_pass(0, 3)
-
         weave_x(vec, 1, 2)
         weave_x(act, 1, 3)
         round_z(0)
-        quantize_x(1, 2)
-        z_pass(1, 2)
-        quantize_x(1, 3)
-        z_pass(1, 3)
-        weave_w(vec, 0, 0)
+        for i in (2, 3):
+            quantize_x(1, i)
+            z_pass(1, i)
+
         weave_w(act, 1, 0)
         quantize_z(0)
-        low_products(0, 0)
-        low_products(0, 1)
+        for pair in range(2):
+            low_products(0, pair)
+        weave_w(vec, 0, 0)
         round_z(1)
-        w_pass(0, 0)
-        copy_low(0, 0)
         turn_bias()
         w_pass(1, 0)
+        w_pass(0, 0)
+        copy_bank(vec, 0, 0)
+        copy_bank(act, 0, 2)
         quantize_z(1)
         copy_low(0, 1)
-        low_products(1, 0)
-        low_products(1, 1)
-
-        weave_w(vec, 0, 1)
-        weave_w(vec, 1, 1)
-        w_pass(0, 1)
-        w_pass(1, 1)
-        copy_low(1, 0)
-        weave_w(act, 3, 0)
+        weave_w(act, 1, 1, 0, SHARED)
+        for pair in range(2):
+            low_products(1, pair)
 
         last = TILES - 1
+        weave_w(vec, 0, 1)
+        weave_w(vec, 1, 1, SHARED, P)
+        w_pass(0, 1)
+        copy_low(1, 0)
         weave_w(vec, 2, 0)
+        w_pass(1, 1)
+        copy_bank(vec, 1, 1)
         weave_w(act, 2, 1)
+        weave_w(act, last, 0)
         w_pass(2, 0)
         add(0, 0, 2)
-        finish(0, 0, 2)
-        quantize_w(last, 0)
         add(0, 2, 4)
-        finish(0, 2, 4)
-        weave_w(vec, last, 1)
         w_pass(2, 1)
-        copy_low(1, 1)
-        main_pass(last, 0, 0, 2)
-        main_pass(last, 0, 2, 4)
         add(1, 0, 2)
+        finish(0, 0, 2)
+        finish(0, 2, 4)
+
+        weave_w(vec, last, 1)
+        finish(1, 0, 2)
+        copy_bank(act, 1, 3)
+        quantize_w(last, 0)
+        main_pass(last, 0, 0, 2)
+        add(1, 2, 4)
         quantize_w(last, 1)
         main_pass(last, 1, 0, 2)
-        main_pass(last, 1, 2, 4)
-        finish(1, 0, 2)
-        for t, lo, hi, first in ((1, 2, 4, 0), (2, 0, 2, 0), (2, 2, 4, 0), (last, 0, 2, 0), (last, 2, 3, 2), (last, 3, 4, 2)):
+        for c in range(PASSES):
+            main_pass(last, c, 2, 4)
+        finish(1, 2, 4)
+
+        for t, lo, hi, first in ((2, 0, 2, 0), (2, 2, 4, 0), (last, 0, 2, 0), (last, 2, 3, 2), (last, 3, 4, 2)):
             add(t, lo, hi, first)
             finish(t, lo, hi)

@@ -28,6 +28,7 @@ A_WIDTH = PACK * P + SIDE
 BB_WORDS = P + P // 4
 BIAS_STEP = P // (TILES * QUADS)
 SHARED = P // 2
+WARM_UPS = 8
 WHOLE_BANKS = 4
 
 
@@ -231,6 +232,12 @@ def tile_rows_lora_tanh_bias_kernel(tc, x, w, a, bb, b, out):
 
         quantize_a(0)
         spread_a(0)
+
+        warm = whole_psum.tile([P, CHUNK], F32, name="warm", tag="whole")
+        warm_codes = a_codes[0][:].rearrange("p s d -> p (s d)").bitcast(FP8X4)
+        for i in range(WARM_UPS):
+            nc.tensor.matmul_mx(out=warm[:], lhsT=warm_codes, lhsT_scale=a_scales[0][:], rhs=warm_codes, rhs_scale=a_scales[0][:],
+                                start=True, stop=True)
 
         weave_x(vec, 0, 0)
         for i in range(1, CHUNKS):

@@ -28,6 +28,7 @@ A_WIDTH = PACK * P + SIDE
 BB_WORDS = P + P // 4
 BIAS_STEP = P // (TILES * QUADS)
 SHARED = P // 2
+X_SHARE = 88
 WARM_UPS = 8
 WHOLE_BANKS = 4
 
@@ -93,13 +94,17 @@ def tile_rows_lora_tanh_bias_kernel(tc, x, w, a, bb, b, out):
                             in_=bb[:, t * P:(t + 1) * P].rearrange("(p j) m -> p j m", j=PACK))
 
         def load_a(c):
-            nc.sync.dma_start(out=a_raw[c][:], in_=a[k_rows(c), :].rearrange("(p j) r -> p j r", j=PACK))
+            (nc.sync, nc.scalar)[c].dma_start(out=a_raw[c][:], in_=a[k_rows(c), :].rearrange("(p j) r -> p j r", j=PACK))
 
         def load_columns(name, src, raw, c, lo, hi):
             both = sb("%s_raw%d%d" % (name, c, lo), [P, PACK, (hi - lo) * CHUNK], F32)
             nc.sync.dma_start(out=both[:], in_=src[k_rows(c), cols(lo, hi)].rearrange("(p j) n -> p j n", j=PACK))
             for i in range(lo, hi):
-                raw[c, i] = both[:, :, cols(i - lo, i - lo + 1)]
+                raw[c, i] = (both, lo * CHUNK)
+
+        def raw_columns(raw, c, lo, hi):
+            tile, first = raw[c, lo // CHUNK]
+            return tile[:, :, lo - first:hi - first]
 
         def load_x(c, lo, hi):
             load_columns("x", x, x_raw, c, lo, hi)
@@ -108,7 +113,7 @@ def tile_rows_lora_tanh_bias_kernel(tc, x, w, a, bb, b, out):
             load_columns("w", w, w_raw, c, lo, hi)
 
         def load_bias():
-            nc.sync.dma_start(out=bias_rows[0:P:BIAS_STEP, :], in_=b.rearrange("(t q i) o -> q t (i o)", t=TILES, i=QUAD))
+            nc.scalar.dma_start(out=bias_rows[0:P:BIAS_STEP, :], in_=b.rearrange("(t q i) o -> q t (i o)", t=TILES, i=QUAD))
 
         def turn_bias():
             nc.vector.transpose(out=bias[:], in_=bias_rows[:])
@@ -132,11 +137,13 @@ def tile_rows_lora_tanh_bias_kernel(tc, x, w, a, bb, b, out):
                 groups = dst[:, 0:PACK * P].bitcast(I32).rearrange("p (s q i) -> p s q i", q=QUADS, i=width)
                 nc.vector.tensor_copy(out=groups[:, :, 2:QUADS, :], in_=src.unsqueeze(2).to_broadcast([P, PACK, 2, width]))
 
-        def weave_x(copy, c, i):
-            weave(copy, x_bf[c][:, cols(i, i + 1), :], x_raw[c, i])
+        def weave_x(copy, c, i, lo=0, hi=CHUNK):
+            lo, hi = i * CHUNK + lo, i * CHUNK + hi
+            weave(copy, x_bf[c][:, lo:hi, :], raw_columns(x_raw, c, lo, hi))
 
-        def quantize_x(c, i):
-            quantize(x_codes[c][:, cols(i, i + 1)], x_scales[c][:, cols(i, i + 1)], x_bf[c][:, cols(i, i + 1), :])
+        def quantize_x(c, i, count=1):
+            span = cols(i, i + count)
+            quantize(x_codes[c][:, span], x_scales[c][:, span], x_bf[c][:, span, :])
 
         def z_pass(c, i):
             h, side = divmod(i, 2)
@@ -175,7 +182,7 @@ def tile_rows_lora_tanh_bias_kernel(tc, x, w, a, bb, b, out):
                 copy_bank(act, h, q)
 
         def weave_w(copy, t, c, lo=0, hi=P):
-            weave(copy, w_bf[t][:, c, lo:hi, :], w_raw[c, t][:, :, lo:hi])
+            weave(copy, w_bf[t][:, c, lo:hi, :], raw_columns(w_raw, c, t * P + lo, t * P + hi))
 
         def quantize_w(t, c):
             quantize(w_codes[t][:, c * P:(c + 1) * P], w_scales[t][:, c * P:(c + 1) * P], w_bf[t][:, c, :, :])
@@ -214,9 +221,10 @@ def tile_rows_lora_tanh_bias_kernel(tc, x, w, a, bb, b, out):
 
         for q in (0, 2, 1, 3):
             load_bb(q)
-        load_a(0)
+        for c in range(PASSES):
+            load_a(c)
+        load_bias()
         load_x(0, 0, CHUNKS)
-        load_a(1)
         for h in range(HALVES):
             load_x(1, 2 * h, 2 * h + 2)
         weave(vec, bb_bf[:], bb_raw[:])
@@ -224,43 +232,38 @@ def tile_rows_lora_tanh_bias_kernel(tc, x, w, a, bb, b, out):
         quantize_bb()
         load_w(0, 0, 2)
         swap_bb()
-        load_bias()
         load_w(1, 0, 2)
         for t in range(2, TILES):
             for c in range(PASSES):
                 load_w(c, t, t + 1)
-
-        quantize_a(0)
-        spread_a(0)
-
-        warm = whole_psum.tile([P, CHUNK], F32, name="warm", tag="whole")
-        warm_codes = a_codes[0][:].rearrange("p s d -> p (s d)").bitcast(FP8X4)
-        for i in range(WARM_UPS):
-            nc.tensor.matmul_mx(out=warm[:], lhsT=warm_codes, lhsT_scale=a_scales[0][:], rhs=warm_codes, rhs_scale=a_scales[0][:],
-                                start=True, stop=True)
-
-        weave_x(vec, 0, 0)
-        for i in range(1, CHUNKS):
-            weave_x(act, 0, i)
-        quantize_x(0, 0)
-        z_pass(0, 0)
         weave_a(vec, 1)
-        quantize_x(0, 1)
-        z_pass(0, 1)
+        quantize_a(0)
         quantize_a(1)
-        quantize_x(0, 2)
-        z_pass(0, 2)
+        spread_a(0)
         spread_a(1)
-
-        weave_x(vec, 1, 0)
-        weave_x(act, 1, 1)
+        warm = whole_psum.tile([P, CHUNK], F32, name="warm", tag="whole")
+        warm_codes, warm_scales = win_codes[1][:, SIDE:SIDE + P].bitcast(FP8X4), win_scales[1][:, SIDE:SIDE + P]
+        for i in range(WARM_UPS):
+            nc.tensor.matmul_mx(out=warm[:], lhsT=warm_codes, lhsT_scale=warm_scales, rhs=warm_codes, rhs_scale=warm_scales,
+                                start=True, stop=True)
+        weave_x(vec, 0, 0)
+        weave_x(act, 0, 2)
+        weave_x(vec, 0, 1)
+        weave_x(act, 0, 3)
+        for i in (0, 1, 2):
+            quantize_x(0, i)
+            z_pass(0, i)
+        for i in (0, 1):
+            weave_x(vec, 1, i, 0, X_SHARE)
+            weave_x(act, 1, i, X_SHARE, CHUNK)
         quantize_x(0, 3)
         for i in (0, 1):
             quantize_x(1, i)
             z_pass(1, i)
         z_pass(0, 3)
-        weave_x(vec, 1, 2)
-        weave_x(act, 1, 3)
+        for i in (2, 3):
+            weave_x(vec, 1, i, 0, X_SHARE)
+            weave_x(act, 1, i, X_SHARE, CHUNK)
         round_z(0)
         for i in (2, 3):
             quantize_x(1, i)
@@ -302,17 +305,17 @@ def tile_rows_lora_tanh_bias_kernel(tc, x, w, a, bb, b, out):
         finish(0, 2, 4)
 
         weave_w(vec, last, 1)
-        finish(1, 0, 2)
         copy_bank(act, 1, 3)
+        finish(1, 0, 2)
         quantize_w(last, 0)
         main_pass(last, 0, 0, 2)
         add(1, 2, 4)
+        main_pass(last, 0, 2, 4)
         quantize_w(last, 1)
         main_pass(last, 1, 0, 2)
-        for c in range(PASSES):
-            main_pass(last, c, 2, 4)
+        main_pass(last, 1, 2, 4)
         finish(1, 2, 4)
 
-        for t, lo, hi, first in ((2, 0, 2, 0), (2, 2, 4, 0), (last, 0, 2, 0), (last, 2, 3, 2), (last, 3, 4, 2)):
+        for t, lo, hi, first in ((2, 0, 2, 0), (2, 2, 4, 0), (last, 0, 1, 0), (last, 1, 2, 0), (last, 2, 3, 2), (last, 3, 4, 2)):
             add(t, lo, hi, first)
             finish(t, lo, hi)

@@ -96,9 +96,12 @@ def tile_rows_lora_tanh_bias_kernel(tc, x, w, a, bb, b, out):
         def load_a(c):
             (nc.sync, nc.scalar)[c].dma_start(out=a_raw[c][:], in_=a[k_rows(c), :].rearrange("(p j) r -> p j r", j=PACK))
 
-        def load_columns(name, src, raw, c, lo, hi):
+        def load_columns(name, src, raw, c, lo, hi, queues):
             both = sb("%s_raw%d%d" % (name, c, lo), [P, PACK, (hi - lo) * CHUNK], F32)
-            nc.sync.dma_start(out=both[:], in_=src[k_rows(c), cols(lo, hi)].rearrange("(p j) n -> p j n", j=PACK))
+            rows = src[k_rows(c), cols(lo, hi)].rearrange("(p j) n -> p j n", j=PACK)
+            share = PACK // len(queues)
+            for i, queue in enumerate(queues):
+                queue.dma_start(out=both[:, i * share:(i + 1) * share, :], in_=rows[:, i * share:(i + 1) * share, :])
             for i in range(lo, hi):
                 raw[c, i] = (both, lo * CHUNK)
 
@@ -107,13 +110,13 @@ def tile_rows_lora_tanh_bias_kernel(tc, x, w, a, bb, b, out):
             return tile[:, :, lo - first:hi - first]
 
         def load_x(c, lo, hi):
-            load_columns("x", x, x_raw, c, lo, hi)
+            load_columns("x", x, x_raw, c, lo, hi, (nc.sync, nc.scalar))
 
-        def load_w(c, lo, hi):
-            load_columns("w", w, w_raw, c, lo, hi)
+        def load_w(c, lo, hi, queues=(nc.sync,)):
+            load_columns("w", w, w_raw, c, lo, hi, queues)
 
         def load_bias():
-            nc.scalar.dma_start(out=bias_rows[0:P:BIAS_STEP, :], in_=b.rearrange("(t q i) o -> q t (i o)", t=TILES, i=QUAD))
+            nc.sync.dma_start(out=bias_rows[0:P:BIAS_STEP, :], in_=b.rearrange("(t q i) o -> q t (i o)", t=TILES, i=QUAD))
 
         def turn_bias():
             nc.vector.transpose(out=bias[:], in_=bias_rows[:])
@@ -223,7 +226,6 @@ def tile_rows_lora_tanh_bias_kernel(tc, x, w, a, bb, b, out):
             load_bb(q)
         for c in range(PASSES):
             load_a(c)
-        load_bias()
         load_x(0, 0, CHUNKS)
         for h in range(HALVES):
             load_x(1, 2 * h, 2 * h + 2)
@@ -233,19 +235,20 @@ def tile_rows_lora_tanh_bias_kernel(tc, x, w, a, bb, b, out):
         load_w(0, 0, 2)
         swap_bb()
         load_w(1, 0, 2)
+        load_bias()
         for t in range(2, TILES):
             for c in range(PASSES):
                 load_w(c, t, t + 1)
         weave_a(vec, 1)
-        quantize_a(0)
         quantize_a(1)
-        spread_a(0)
         spread_a(1)
         warm = whole_psum.tile([P, CHUNK], F32, name="warm", tag="whole")
         warm_codes, warm_scales = win_codes[1][:, SIDE:SIDE + P].bitcast(FP8X4), win_scales[1][:, SIDE:SIDE + P]
         for i in range(WARM_UPS):
             nc.tensor.matmul_mx(out=warm[:], lhsT=warm_codes, lhsT_scale=warm_scales, rhs=warm_codes, rhs_scale=warm_scales,
                                 start=True, stop=True)
+        quantize_a(0)
+        spread_a(0)
         weave_x(vec, 0, 0)
         weave_x(act, 0, 2)
         weave_x(vec, 0, 1)
@@ -275,7 +278,6 @@ def tile_rows_lora_tanh_bias_kernel(tc, x, w, a, bb, b, out):
             low_products(0, pair)
         weave_w(vec, 0, 0)
         round_z(1)
-        turn_bias()
         w_pass(1, 0)
         w_pass(0, 0)
         copy_bank(vec, 0, 0)
@@ -289,6 +291,7 @@ def tile_rows_lora_tanh_bias_kernel(tc, x, w, a, bb, b, out):
         last = TILES - 1
         weave_w(vec, 0, 1)
         weave_w(vec, 1, 1, SHARED, P)
+        turn_bias()
         w_pass(0, 1)
         copy_low(1, 0)
         weave_w(vec, 2, 0)

@@ -36,6 +36,7 @@ WHOLE_BANKS = 4
 def tile_rows_lora_tanh_bias_kernel(tc, x, w, a, bb, b, out):
     nc = tc.nc
     vec, act = nc.vector.tensor_copy, nc.scalar.copy
+    queues = (nc.sync, nc.scalar)
     with ExitStack() as ctx:
         keep = ctx.enter_context(tc.tile_pool(name="keep", bufs=1))
         whole_psum = ctx.enter_context(tc.psum_pool(name="whole_psum", bufs=WHOLE_BANKS))
@@ -89,19 +90,19 @@ def tile_rows_lora_tanh_bias_kernel(tc, x, w, a, bb, b, out):
 
         def load_bb(q):
             t = 2 * (q % 2) + q // 2
-            queue = nc.sync if q < 2 else nc.scalar
-            queue.dma_start(out=bb_raw[QUAD * q:QUAD * (q + 1), :, :],
-                            in_=bb[:, t * P:(t + 1) * P].rearrange("(p j) m -> p j m", j=PACK))
+            queues[q // 2].dma_start(out=bb_raw[QUAD * q:QUAD * (q + 1), :, :],
+                                     in_=bb[:, t * P:(t + 1) * P].rearrange("(p j) m -> p j m", j=PACK))
 
         def load_a(c):
-            (nc.sync, nc.scalar)[c].dma_start(out=a_raw[c][:], in_=a[k_rows(c), :].rearrange("(p j) r -> p j r", j=PACK))
+            queues[c].dma_start(out=a_raw[c][:], in_=a[k_rows(c), :].rearrange("(p j) r -> p j r", j=PACK))
 
-        def load_columns(name, src, raw, c, lo, hi, queues):
+        def load_columns(name, src, raw, c, lo, hi, parts):
             both = sb("%s_raw%d%d" % (name, c, lo), [P, PACK, (hi - lo) * CHUNK], F32)
             rows = src[k_rows(c), cols(lo, hi)].rearrange("(p j) n -> p j n", j=PACK)
-            share = PACK // len(queues)
-            for i, queue in enumerate(queues):
-                queue.dma_start(out=both[:, i * share:(i + 1) * share, :], in_=rows[:, i * share:(i + 1) * share, :])
+            share = PACK // parts
+            for part in range(parts):
+                own = slice(part * share, (part + 1) * share)
+                queues[part].dma_start(out=both[:, own, :], in_=rows[:, own, :])
             for i in range(lo, hi):
                 raw[c, i] = (both, lo * CHUNK)
 
@@ -110,10 +111,10 @@ def tile_rows_lora_tanh_bias_kernel(tc, x, w, a, bb, b, out):
             return tile[:, :, lo - first:hi - first]
 
         def load_x(c, lo, hi):
-            load_columns("x", x, x_raw, c, lo, hi, (nc.sync, nc.scalar))
+            load_columns("x", x, x_raw, c, lo, hi, len(queues))
 
-        def load_w(c, lo, hi, queues=(nc.sync,)):
-            load_columns("w", w, w_raw, c, lo, hi, queues)
+        def load_w(c, lo, hi):
+            load_columns("w", w, w_raw, c, lo, hi, 1)
 
         def load_bias():
             nc.sync.dma_start(out=bias_rows[0:P:BIAS_STEP, :], in_=b.rearrange("(t q i) o -> q t (i o)", t=TILES, i=QUAD))
@@ -141,11 +142,14 @@ def tile_rows_lora_tanh_bias_kernel(tc, x, w, a, bb, b, out):
                 nc.vector.tensor_copy(out=groups[:, :, 2:QUADS, :], in_=src.unsqueeze(2).to_broadcast([P, PACK, 2, width]))
 
         def weave_x(copy, c, i, lo=0, hi=CHUNK):
-            lo, hi = i * CHUNK + lo, i * CHUNK + hi
-            weave(copy, x_bf[c][:, lo:hi, :], raw_columns(x_raw, c, lo, hi))
+            weave(copy, x_bf[c][:, i * CHUNK + lo:i * CHUNK + hi, :], raw_columns(x_raw, c, i * CHUNK + lo, i * CHUNK + hi))
 
-        def quantize_x(c, i, count=1):
-            span = cols(i, i + count)
+        def share_x(c, i):
+            weave_x(vec, c, i, 0, X_SHARE)
+            weave_x(act, c, i, X_SHARE, CHUNK)
+
+        def quantize_x(c, i):
+            span = cols(i, i + 1)
             quantize(x_codes[c][:, span], x_scales[c][:, span], x_bf[c][:, span, :])
 
         def z_pass(c, i):
@@ -239,47 +243,52 @@ def tile_rows_lora_tanh_bias_kernel(tc, x, w, a, bb, b, out):
         for t in range(2, TILES):
             for c in range(PASSES):
                 load_w(c, t, t + 1)
+
         weave_a(vec, 1)
         quantize_a(1)
         spread_a(1)
+
         warm = whole_psum.tile([P, CHUNK], F32, name="warm", tag="whole")
         warm_codes, warm_scales = win_codes[1][:, SIDE:SIDE + P].bitcast(FP8X4), win_scales[1][:, SIDE:SIDE + P]
         for i in range(WARM_UPS):
             nc.tensor.matmul_mx(out=warm[:], lhsT=warm_codes, lhsT_scale=warm_scales, rhs=warm_codes, rhs_scale=warm_scales,
                                 start=True, stop=True)
+
         quantize_a(0)
         spread_a(0)
+
         weave_x(vec, 0, 0)
         weave_x(act, 0, 2)
         weave_x(vec, 0, 1)
         weave_x(act, 0, 3)
-        for i in (0, 1, 2):
+        for i in (0, 1):
             quantize_x(0, i)
             z_pass(0, i)
+        quantize_x(0, 2)
+
         for i in (0, 1):
-            weave_x(vec, 1, i, 0, X_SHARE)
-            weave_x(act, 1, i, X_SHARE, CHUNK)
+            share_x(1, i)
         quantize_x(0, 3)
         for i in (0, 1):
             quantize_x(1, i)
             z_pass(1, i)
+        z_pass(0, 2)
         z_pass(0, 3)
         for i in (2, 3):
-            weave_x(vec, 1, i, 0, X_SHARE)
-            weave_x(act, 1, i, X_SHARE, CHUNK)
+            share_x(1, i)
         round_z(0)
         for i in (2, 3):
             quantize_x(1, i)
             z_pass(1, i)
 
         weave_w(act, 1, 0)
+        weave_w(vec, 0, 0)
         quantize_z(0)
         for pair in range(2):
             low_products(0, pair)
-        weave_w(vec, 0, 0)
         round_z(1)
-        w_pass(1, 0)
         w_pass(0, 0)
+        w_pass(1, 0)
         copy_bank(vec, 0, 0)
         copy_bank(act, 0, 2)
         quantize_z(1)

@@ -213,10 +213,16 @@ def tile_rows_lora_tanh_bias_kernel(tc, x, w, a, bb, b, out):
                                     in0=y_bank[t, first][:, cols(lo - first, hi - first)].rearrange("p (i n) -> p i n", n=CHUNK),
                                     in1=low[t // 2][:, lo:hi, t % 2, :], op=mybir.AluOpType.add)
 
-        def finish(t, lo, hi):
+        def squash(t, lo, hi):
             nc.scalar.activation(out=res[t][:, cols(lo, hi)], in_=pre[t][:, cols(lo, hi)], func=ACT.Tanh,
                                  bias=bias[:, BIAS_STEP * t:BIAS_STEP * t + 1])
+
+        def store(t, lo, hi):
             nc.sync.dma_start(out=out[t * P:(t + 1) * P, cols(lo, hi)], in_=res[t][:, cols(lo, hi)])
+
+        def finish(t, lo, hi):
+            squash(t, lo, hi)
+            store(t, lo, hi)
 
         nc.gpsimd.memset(bb_own[:, P:BB_WORDS].bitcast(I32), 0)
         for c in range(PASSES):
@@ -328,6 +334,11 @@ def tile_rows_lora_tanh_bias_kernel(tc, x, w, a, bb, b, out):
         main_pass(last, 1, 2, 4)
         finish(1, 2, 4)
 
-        for t, lo, hi, first in ((2, 0, 2, 0), (2, 2, 4, 0), (last, 0, 1, 0), (last, 1, 2, 0), (last, 2, 3, 2), (last, 3, 4, 2)):
-            add(t, lo, hi, first)
-            finish(t, lo, hi)
+        for lo in (0, 2):
+            add(2, lo, lo + 2)
+            finish(2, lo, lo + 2)
+        for lo in (0, 2):
+            for i in (lo, lo + 1):
+                add(last, i, i + 1, lo)
+                squash(last, i, i + 1)
+            store(last, lo, lo + 2)

@@ -29,7 +29,7 @@ BB_WORDS = P + P // 4
 BIAS_STEP = P // (TILES * QUADS)
 SHARED = P // 2
 X_SHARE = 88
-WARM_UPS = 8
+WARM_UPS = 6
 WHOLE_BANKS = 4
 
 

@@ -27,10 +27,8 @@ RUN = 4
 A_WIDTH = PACK * P + SIDE
 BB_WORDS = P + P // 4
 BIAS_STEP = P // (TILES * QUADS)
-SHARED = P // 2
 X_SHARE = 88
 WARM_UPS = 6
-WHOLE_BANKS = 4
 
 
 def tile_rows_lora_tanh_bias_kernel(tc, x, w, a, bb, b, out):
@@ -39,12 +37,14 @@ def tile_rows_lora_tanh_bias_kernel(tc, x, w, a, bb, b, out):
     queues = (nc.sync, nc.scalar)
     with ExitStack() as ctx:
         keep = ctx.enter_context(tc.tile_pool(name="keep", bufs=1))
-        whole_psum = ctx.enter_context(tc.psum_pool(name="whole_psum", bufs=WHOLE_BANKS))
-        row_psum = ctx.enter_context(tc.psum_pool(name="row_psum", bufs=1))
+        psum = ctx.enter_context(tc.psum_pool(name="psum", bufs=1))
         ctx.enter_context(tc.manual_schedule())
 
         def sb(name, shape, dtype):
             return keep.tile(shape, dtype, name=name, align_bytes=64)
+
+        def whole_bank(name, slot, shape):
+            return psum.tile(shape, F32, name=name, tag="whole%d" % slot)
 
         def k_rows(c):
             return slice(c * P * PACK, (c + 1) * P * PACK)
@@ -78,7 +78,7 @@ def tile_rows_lora_tanh_bias_kernel(tc, x, w, a, bb, b, out):
         low = [sb("low%d" % pair, [P, CHUNKS, 2, CHUNK], F32) for pair in range(2)]
         pre = [sb("pre%d" % t, [P, N], F32) for t in range(TILES)]
         res = [sb("res%d" % t, [P, N], F32) for t in range(TILES)]
-        low_bank = [row_psum.tile([P, N], F32, name="low_bank%d" % q) for q in range(QUADS)]
+        low_bank = [psum.tile([P, N], F32, name="low_bank%d" % q) for q in range(QUADS)]
         z_bank = {}
         y_bank = {}
 
@@ -110,8 +110,8 @@ def tile_rows_lora_tanh_bias_kernel(tc, x, w, a, bb, b, out):
             tile, first = raw[c, lo // CHUNK]
             return tile[:, :, lo - first:hi - first]
 
-        def load_x(c, lo, hi):
-            load_columns("x", x, x_raw, c, lo, hi, len(queues))
+        def load_x(c, lo, hi, parts):
+            load_columns("x", x, x_raw, c, lo, hi, parts)
 
         def load_w(c, lo, hi):
             load_columns("w", w, w_raw, c, lo, hi, 1)
@@ -155,7 +155,7 @@ def tile_rows_lora_tanh_bias_kernel(tc, x, w, a, bb, b, out):
         def z_pass(c, i):
             h, side = divmod(i, 2)
             if h not in z_bank:
-                z_bank[h] = whole_psum.tile([P, PACK, CHUNK], F32, name="z_bank%d" % h, tag="whole")
+                z_bank[h] = whole_bank("z_bank%d" % h, 1 + h, [P, PACK, CHUNK])
             for s in range(PACK):
                 at = s * P + (1 - side) * SIDE
                 nc.tensor.matmul_mx(
@@ -170,16 +170,22 @@ def tile_rows_lora_tanh_bias_kernel(tc, x, w, a, bb, b, out):
         def quantize_z(h):
             quantize(z_codes[h][:], z_scales[h][:], z_bf[h][:])
 
+        def low_product(h, q, u):
+            rows = slice(QUAD * q, QUAD * (q + 1))
+            src = bb_own if q // 2 == u else bb_far
+            nc.tensor.matmul_mx(
+                out=low_bank[q][:, cols(2 * h + u, 2 * h + u + 1)],
+                lhsT=src[rows, 0:P].bitcast(FP8X4), lhsT_scale=src[rows, P:BB_WORDS].bitcast(U8),
+                rhs=z_codes[h][rows, :].bitcast(FP8X4), rhs_scale=z_scales[h][rows, :],
+                start=True, stop=True)
+
         def low_products(h, pair):
             for u in range(2):
                 for q in (pair, pair + 2):
-                    rows = slice(QUAD * q, QUAD * (q + 1))
-                    src = bb_own if q // 2 == u else bb_far
-                    nc.tensor.matmul_mx(
-                        out=low_bank[q][:, cols(2 * h + u, 2 * h + u + 1)],
-                        lhsT=src[rows, 0:P].bitcast(FP8X4), lhsT_scale=src[rows, P:BB_WORDS].bitcast(U8),
-                        rhs=z_codes[h][rows, :].bitcast(FP8X4), rhs_scale=z_scales[h][rows, :],
-                        start=True, stop=True)
+                    low_product(h, q, u)
+
+        def copy_tile(copy, h, q, u):
+            copy(out=low[q % 2][:, 2 * h + q // 2, u, :], in_=low_bank[q][:, cols(2 * h + u, 2 * h + u + 1)])
 
         def copy_bank(copy, h, q):
             copy(out=low[q % 2][:, 2 * h + q // 2, :, :].rearrange("p u n -> p (u n)"), in_=low_bank[q][:, cols(2 * h, 2 * h + 2)])
@@ -194,19 +200,15 @@ def tile_rows_lora_tanh_bias_kernel(tc, x, w, a, bb, b, out):
         def quantize_w(t, c):
             quantize(w_codes[t][:, c * P:(c + 1) * P], w_scales[t][:, c * P:(c + 1) * P], w_bf[t][:, c, :, :])
 
-        def main_pass(t, c, lo, hi):
+        def main_pass(t, c, lo, hi, slot=None):
             if c == 0:
-                y_bank[t, lo] = whole_psum.tile([P, (hi - lo) * CHUNK], F32, name="y_bank%d%d" % (t, lo), tag="whole")
+                y_bank[t, lo] = whole_bank("y_bank%d%d" % (t, lo), slot, [P, (hi - lo) * CHUNK])
             for i in range(lo, hi):
                 nc.tensor.matmul_mx(
                     out=y_bank[t, lo][:, cols(i - lo, i - lo + 1)],
                     lhsT=w_codes[t][:, c * P:(c + 1) * P].bitcast(FP8X4), lhsT_scale=w_scales[t][:, c * P:(c + 1) * P],
                     rhs=x_codes[c][:, cols(i, i + 1)].bitcast(FP8X4), rhs_scale=x_scales[c][:, cols(i, i + 1)],
                     start=(c == 0 and i == lo), stop=(c == PASSES - 1 and i == hi - 1))
-
-        def w_pass(t, c):
-            quantize_w(t, c)
-            main_pass(t, c, 0, CHUNKS)
 
         def add(t, lo, hi, first=0):
             nc.vector.tensor_tensor(out=pre[t][:, cols(lo, hi)].rearrange("p (i n) -> p i n", n=CHUNK),
@@ -224,6 +226,12 @@ def tile_rows_lora_tanh_bias_kernel(tc, x, w, a, bb, b, out):
             squash(t, lo, hi)
             store(t, lo, hi)
 
+        def warm_up(c):
+            warm = whole_bank("warm", 0, [P, CHUNK])
+            codes, scales = win_codes[c][:, SIDE:SIDE + P].bitcast(FP8X4), win_scales[c][:, SIDE:SIDE + P]
+            for i in range(WARM_UPS):
+                nc.tensor.matmul_mx(out=warm[:], lhsT=codes, lhsT_scale=scales, rhs=codes, rhs_scale=scales, start=True, stop=True)
+
         nc.gpsimd.memset(bb_own[:, P:BB_WORDS].bitcast(I32), 0)
         for c in range(PASSES):
             nc.gpsimd.memset(a_scales[c][:].bitcast(I32), 0)
@@ -236,30 +244,23 @@ def tile_rows_lora_tanh_bias_kernel(tc, x, w, a, bb, b, out):
             load_bb(q)
         for c in range(PASSES):
             load_a(c)
-        load_x(0, 0, CHUNKS)
-        for h in range(HALVES):
-            load_x(1, 2 * h, 2 * h + 2)
+        for c in range(PASSES):
+            load_x(c, 0, CHUNKS, 1)
         weave(vec, bb_bf[:], bb_raw[:])
         weave_a(act, 0)
         quantize_bb()
+        load_bias()
         load_w(0, 0, 2)
         swap_bb()
         load_w(1, 0, 2)
-        load_bias()
-        for t in range(2, TILES):
-            for c in range(PASSES):
-                load_w(c, t, t + 1)
+        load_w(0, 2, 4)
+        load_w(1, 2, 3)
+        load_w(1, 3, 4)
 
         weave_a(vec, 1)
         quantize_a(1)
         spread_a(1)
-
-        warm = whole_psum.tile([P, CHUNK], F32, name="warm", tag="whole")
-        warm_codes, warm_scales = win_codes[1][:, SIDE:SIDE + P].bitcast(FP8X4), win_scales[1][:, SIDE:SIDE + P]
-        for i in range(WARM_UPS):
-            nc.tensor.matmul_mx(out=warm[:], lhsT=warm_codes, lhsT_scale=warm_scales, rhs=warm_codes, rhs_scale=warm_scales,
-                                start=True, stop=True)
-
+        warm_up(1)
         quantize_a(0)
         spread_a(0)
 
@@ -267,78 +268,79 @@ def tile_rows_lora_tanh_bias_kernel(tc, x, w, a, bb, b, out):
         weave_x(act, 0, 2)
         weave_x(vec, 0, 1)
         weave_x(act, 0, 3)
-        for i in (0, 1):
+        for i in range(CHUNKS):
             quantize_x(0, i)
             z_pass(0, i)
-        quantize_x(0, 2)
-
-        for i in (0, 1):
-            share_x(1, i)
-        quantize_x(0, 3)
-        for i in (0, 1):
-            quantize_x(1, i)
-            z_pass(1, i)
-        z_pass(0, 2)
-        z_pass(0, 3)
-        for i in (2, 3):
-            share_x(1, i)
-        round_z(0)
-        for i in (2, 3):
-            quantize_x(1, i)
-            z_pass(1, i)
-
+        share_x(1, 0)
+        share_x(1, 1)
+        weave_x(vec, 1, 2, 0, 56)
+        weave_x(act, 1, 2, 56, 128)
+        quantize_x(1, 0)
+        z_pass(1, 0)
+        quantize_x(1, 1)
+        z_pass(1, 1)
+        weave_x(vec, 1, 3, 0, 80)
+        weave_x(act, 1, 3, 80, 128)
+        quantize_x(1, 2)
+        z_pass(1, 2)
+        turn_bias()
+        quantize_x(1, 3)
+        z_pass(1, 3)
         weave_w(act, 1, 0)
         weave_w(vec, 0, 0)
+        round_z(0)
+        round_z(1)
+        quantize_w(0, 0)
+        main_pass(0, 0, 0, 4, 3)
+        quantize_w(1, 0)
+        main_pass(1, 0, 0, 4, 0)
         quantize_z(0)
         for pair in range(2):
             low_products(0, pair)
-        round_z(1)
-        w_pass(0, 0)
-        w_pass(1, 0)
-        copy_bank(vec, 0, 0)
-        copy_bank(act, 0, 2)
-        quantize_z(1)
-        copy_low(0, 1)
-        weave_w(act, 1, 1, 0, SHARED)
-        for pair in range(2):
-            low_products(1, pair)
-
-        last = TILES - 1
         weave_w(vec, 0, 1)
-        weave_w(vec, 1, 1, SHARED, P)
-        turn_bias()
-        w_pass(0, 1)
-        copy_low(1, 0)
+        weave_w(act, 1, 1, 64, 128)
+        weave_w(vec, 1, 1, 0, 64)
+        copy_low(0, 0)
+        quantize_z(1)
+        quantize_w(0, 1)
+        main_pass(0, 1, 0, 4)
+        quantize_w(1, 1)
+        for q in (0, 2):
+            for u in range(2):
+                low_product(1, q, u)
+        main_pass(1, 1, 0, 4)
+        copy_low(0, 1)
         weave_w(vec, 2, 0)
-        w_pass(1, 1)
-        copy_bank(vec, 1, 1)
-        weave_w(act, 2, 1)
-        weave_w(act, last, 0)
-        w_pass(2, 0)
+        weave_w(vec, 3, 0)
+        low_products(1, 1)
+        copy_low(1, 0)
+        quantize_w(2, 0)
+        main_pass(2, 0, 0, 4, 1)
+        weave_w(vec, 2, 1)
         add(0, 0, 2)
-        add(0, 2, 4)
-        w_pass(2, 1)
-        add(1, 0, 2)
+        quantize_w(2, 1)
+        main_pass(2, 1, 0, 4)
+        copy_bank(act, 1, 1)
         finish(0, 0, 2)
-        finish(0, 2, 4)
-
-        weave_w(vec, last, 1)
+        weave_w(vec, 3, 1)
+        quantize_w(3, 0)
+        main_pass(3, 0, 0, 2, 2)
+        add(0, 2, 4)
         copy_bank(act, 1, 3)
-        finish(1, 0, 2)
-        quantize_w(last, 0)
-        main_pass(last, 0, 0, 2)
+        finish(0, 2, 4)
+        add(1, 0, 2)
+        quantize_w(3, 1)
+        main_pass(3, 1, 0, 2)
+        main_pass(3, 0, 2, 4, 3)
+        main_pass(3, 1, 2, 4)
         add(1, 2, 4)
-        main_pass(last, 0, 2, 4)
-        quantize_w(last, 1)
-        main_pass(last, 1, 0, 2)
-        main_pass(last, 1, 2, 4)
+        finish(1, 0, 2)
         finish(1, 2, 4)
-
         for lo in (0, 2):
             add(2, lo, lo + 2)
             finish(2, lo, lo + 2)
         for lo in (0, 2):
             for i in (lo, lo + 1):
-                add(last, i, i + 1, lo)
-                squash(last, i, i + 1)
-            store(last, lo, lo + 2)
+                add(3, i, i + 1, lo)
+                squash(3, i, i + 1)
+            store(3, lo, lo + 2)

@@ -250,11 +250,11 @@ def tile_rows_lora_tanh_bias_kernel(tc, x, w, a, bb, b, out):
         weave_a(act, 0)
         quantize_bb()
         load_bias()
-        load_w(0, 0, 2)
+        load_w(0, 0, 3)
         swap_bb()
         load_w(1, 0, 2)
-        load_w(0, 2, 4)
         load_w(1, 2, 3)
+        load_w(0, 3, 4)
         load_w(1, 3, 4)
 
         weave_a(vec, 1)
@@ -286,55 +286,53 @@ def tile_rows_lora_tanh_bias_kernel(tc, x, w, a, bb, b, out):
         turn_bias()
         quantize_x(1, 3)
         z_pass(1, 3)
-        weave_w(act, 1, 0)
-        weave_w(vec, 0, 0)
         round_z(0)
         round_z(1)
+        weave_w(vec, 0, 0)
+        weave_w(vec, 1, 0)
         quantize_w(0, 0)
         main_pass(0, 0, 0, 4, 3)
-        quantize_w(1, 0)
-        main_pass(1, 0, 0, 4, 0)
+        weave_w(vec, 2, 0)
         quantize_z(0)
         for pair in range(2):
             low_products(0, pair)
+        quantize_w(1, 0)
+        main_pass(1, 0, 0, 4, 0)
+        quantize_w(2, 0)
+        main_pass(2, 0, 0, 4, 1)
         weave_w(vec, 0, 1)
-        weave_w(act, 1, 1, 64, 128)
-        weave_w(vec, 1, 1, 0, 64)
-        copy_low(0, 0)
+        weave_w(act, 1, 1)
         quantize_z(1)
         quantize_w(0, 1)
         main_pass(0, 1, 0, 4)
-        quantize_w(1, 1)
+        copy_low(0, 0)
         for q in (0, 2):
             for u in range(2):
                 low_product(1, q, u)
-        main_pass(1, 1, 0, 4)
         copy_low(0, 1)
-        weave_w(vec, 2, 0)
-        weave_w(vec, 3, 0)
+        weave_w(vec, 2, 1)
+        quantize_w(1, 1)
+        main_pass(1, 1, 0, 4)
         low_products(1, 1)
         copy_low(1, 0)
-        quantize_w(2, 0)
-        main_pass(2, 0, 0, 4, 1)
-        weave_w(vec, 2, 1)
-        add(0, 0, 2)
         quantize_w(2, 1)
         main_pass(2, 1, 0, 4)
-        copy_bank(act, 1, 1)
-        finish(0, 0, 2)
-        weave_w(vec, 3, 1)
+        weave_w(vec, 3, 0)
+        add(0, 0, 2)
         quantize_w(3, 0)
         main_pass(3, 0, 0, 2, 2)
-        add(0, 2, 4)
-        copy_bank(act, 1, 3)
-        finish(0, 2, 4)
+        finish(0, 0, 2)
+        weave_w(vec, 3, 1)
         add(1, 0, 2)
+        copy_low(1, 1)
+        finish(1, 0, 2)
+        add(0, 2, 4)
         quantize_w(3, 1)
         main_pass(3, 1, 0, 2)
         main_pass(3, 0, 2, 4, 3)
         main_pass(3, 1, 2, 4)
         add(1, 2, 4)
-        finish(1, 0, 2)
+        finish(0, 2, 4)
         finish(1, 2, 4)
         for lo in (0, 2):
             add(2, lo, lo + 2)

@@ -28,7 +28,6 @@ A_WIDTH = PACK * P + SIDE
 BB_WORDS = P + P // 4
 BIAS_STEP = P // (TILES * QUADS)
 X_SHARE = 88
-WARM_UPS = 6
 
 
 def tile_rows_lora_tanh_bias_kernel(tc, x, w, a, bb, b, out):
@@ -226,12 +225,6 @@ def tile_rows_lora_tanh_bias_kernel(tc, x, w, a, bb, b, out):
             squash(t, lo, hi)
             store(t, lo, hi)
 
-        def warm_up(c):
-            warm = whole_bank("warm", 0, [P, CHUNK])
-            codes, scales = win_codes[c][:, SIDE:SIDE + P].bitcast(FP8X4), win_scales[c][:, SIDE:SIDE + P]
-            for i in range(WARM_UPS):
-                nc.tensor.matmul_mx(out=warm[:], lhsT=codes, lhsT_scale=scales, rhs=codes, rhs_scale=scales, start=True, stop=True)
-
         nc.gpsimd.memset(bb_own[:, P:BB_WORDS].bitcast(I32), 0)
         for c in range(PASSES):
             nc.gpsimd.memset(a_scales[c][:].bitcast(I32), 0)
@@ -260,7 +253,6 @@ def tile_rows_lora_tanh_bias_kernel(tc, x, w, a, bb, b, out):
         weave_a(vec, 1)
         quantize_a(1)
         spread_a(1)
-        warm_up(1)
         quantize_a(0)
         spread_a(0)
 

@@ -290,9 +290,8 @@ def tile_rows_lora_tanh_bias_kernel(tc, x, w, a, bb, b, out):
             low_products(0, pair)
         quantize_w(1, 0)
         main_pass(1, 0, 0, 4, 0)
-        quantize_w(2, 0)
-        main_pass(2, 0, 0, 4, 1)
         weave_w(vec, 0, 1)
+        quantize_w(2, 0)
         weave_w(act, 1, 1)
         quantize_z(1)
         quantize_w(0, 1)
@@ -306,10 +305,11 @@ def tile_rows_lora_tanh_bias_kernel(tc, x, w, a, bb, b, out):
         quantize_w(1, 1)
         main_pass(1, 1, 0, 4)
         low_products(1, 1)
+        main_pass(2, 0, 0, 4, 1)
         copy_low(1, 0)
+        weave_w(vec, 3, 0)
         quantize_w(2, 1)
         main_pass(2, 1, 0, 4)
-        weave_w(vec, 3, 0)
         add(0, 0, 2)
         quantize_w(3, 0)
         main_pass(3, 0, 0, 2, 2)

@@ -240,7 +240,7 @@ def tile_rows_lora_tanh_bias_kernel(tc, x, w, a, bb, b, out):
         for c in range(PASSES):
             load_x(c, 0, CHUNKS, 1)
         weave(vec, bb_bf[:], bb_raw[:])
-        weave_a(act, 0)
+        weave_a(act, 1)
         quantize_bb()
         load_bias()
         load_w(0, 0, 3)
@@ -250,17 +250,19 @@ def tile_rows_lora_tanh_bias_kernel(tc, x, w, a, bb, b, out):
         load_w(0, 3, 4)
         load_w(1, 3, 4)
 
-        weave_a(vec, 1)
-        quantize_a(1)
-        spread_a(1)
+        weave_a(vec, 0)
         quantize_a(0)
+        quantize_a(1)
         spread_a(0)
+        spread_a(1)
 
-        weave_x(vec, 0, 0)
-        weave_x(act, 0, 2)
-        weave_x(vec, 0, 1)
+        share_x(0, 0)
+        share_x(0, 1)
         weave_x(act, 0, 3)
-        for i in range(CHUNKS):
+        quantize_x(0, 0)
+        z_pass(0, 0)
+        weave_x(vec, 0, 2)
+        for i in range(1, CHUNKS):
             quantize_x(0, i)
             z_pass(0, i)
         share_x(1, 0)

from contextlib import ExitStack

import concourse.mybir as mybir

K, R, M, N = 1024, 128, 512, 512
FLOPS = 2 * K * R * N + 2 * K * M * N + 2 * R * M * N

F32 = mybir.dt.float32
BF16 = mybir.dt.bfloat16
U32 = mybir.dt.uint32
I32 = mybir.dt.int32
U8 = mybir.dt.uint8
FP8X4 = mybir.dt.float8_e4m3fn_x4
ACT = mybir.ActivationFunctionType

P = 128
PACK = 4
PASSES = K // (P * PACK)
QUAD = 32
QUADS = P // QUAD
SIDE = P // 2
TILES = M // P
CHUNK = 128
CHUNKS = N // CHUNK
HALVES = CHUNKS // 2
RUN = 4
A_WIDTH = PACK * P + SIDE
BB_WORDS = P + P // 4
BIAS_STEP = P // (TILES * QUADS)
X_SHARE = 88


def tile_rows_lora_tanh_bias_kernel(tc, x, w, a, bb, b, out):
    nc = tc.nc
    vec, act = nc.vector.tensor_copy, nc.scalar.copy
    queues = (nc.sync, nc.scalar)
    with ExitStack() as ctx:
        keep = ctx.enter_context(tc.tile_pool(name="keep", bufs=1))
        psum = ctx.enter_context(tc.psum_pool(name="psum", bufs=1))
        ctx.enter_context(tc.manual_schedule())

        def sb(name, shape, dtype):
            return keep.tile(shape, dtype, name=name, align_bytes=64)

        def whole_bank(name, slot, shape):
            return psum.tile(shape, F32, name=name, tag="whole%d" % slot)

        def k_rows(c):
            return slice(c * P * PACK, (c + 1) * P * PACK)

        def cols(lo, hi):
            return slice(lo * CHUNK, hi * CHUNK)

        a_raw = [sb("a_raw%d" % c, [P, PACK, R], F32) for c in range(PASSES)]
        a_bf = [sb("a_bf%d" % c, [P, PACK, QUAD, PACK], BF16) for c in range(PASSES)]
        a_codes = [sb("a_codes%d" % c, [P, PACK, QUAD], U32) for c in range(PASSES)]
        a_scales = [sb("a_scales%d" % c, [P, PACK * QUAD], U8) for c in range(PASSES)]
        win_codes = [sb("win_codes%d" % c, [P, A_WIDTH], U32) for c in range(PASSES)]
        win_scales = [sb("win_scales%d" % c, [P, A_WIDTH], U8) for c in range(PASSES)]
        bb_raw = sb("bb_raw", [P, PACK, P], F32)
        bb_bf = sb("bb_bf", [P, P, PACK], BF16)
        bb_own = sb("bb_own", [P, BB_WORDS], U32)
        bb_far = sb("bb_far", [P, BB_WORDS], U32)
        bias_rows = sb("bias_rows", [P, QUAD], F32)
        bias = sb("bias", [P, QUAD], F32)
        x_raw = {}
        x_bf = [sb("x_bf%d" % c, [P, N, PACK], BF16) for c in range(PASSES)]
        x_codes = [sb("x_codes%d" % c, [P, N], U32) for c in range(PASSES)]
        x_scales = [sb("x_scales%d" % c, [P, N], U8) for c in range(PASSES)]
        w_raw = {}
        w_bf = [sb("w_bf%d" % t, [P, PASSES, P, PACK], BF16) for t in range(TILES)]
        w_codes = [sb("w_codes%d" % t, [P, PASSES * P], U32) for t in range(TILES)]
        w_scales = [sb("w_scales%d" % t, [P, PASSES * P], U8) for t in range(TILES)]
        z_bf = [sb("z_bf%d" % h, [P, CHUNK, PACK], BF16) for h in range(HALVES)]
        z_codes = [sb("z_codes%d" % h, [P, CHUNK], U32) for h in range(HALVES)]
        z_scales = [sb("z_scales%d" % h, [P, CHUNK], U8) for h in range(HALVES)]
        low = [sb("low%d" % pair, [P, CHUNKS, 2, CHUNK], F32) for pair in range(2)]
        pre = [sb("pre%d" % t, [P, N], F32) for t in range(TILES)]
        res = [sb("res%d" % t, [P, N], F32) for t in range(TILES)]
        low_bank = [psum.tile([P, N], F32, name="low_bank%d" % q) for q in range(QUADS)]
        z_bank = {}
        y_bank = {}

        def weave(copy, dst, src):
            copy(out=dst.rearrange("p (c i) j -> p c j i", i=RUN), in_=src.rearrange("p j (c i) -> p c j i", i=RUN))

        def quantize(codes, scales, src):
            nc.vector.quantize_mx(out=codes.bitcast(FP8X4), scales=scales, in_=src.rearrange("p n j -> p (n j)"))

        def load_bb(q):
            t = 2 * (q % 2) + q // 2
            queues[q // 2].dma_start(out=bb_raw[QUAD * q:QUAD * (q + 1), :, :],
                                     in_=bb[:, t * P:(t + 1) * P].rearrange("(p j) m -> p j m", j=PACK))

        def load_a(c):
            queues[c].dma_start(out=a_raw[c][:], in_=a[k_rows(c), :].rearrange("(p j) r -> p j r", j=PACK))

        def load_columns(name, src, raw, c, lo, hi, parts):
            both = sb("%s_raw%d%d" % (name, c, lo), [P, PACK, (hi - lo) * CHUNK], F32)
            rows = src[k_rows(c), cols(lo, hi)].rearrange("(p j) n -> p j n", j=PACK)
            share = PACK // parts
            for part in range(parts):
                own = slice(part * share, (part + 1) * share)
                queues[part].dma_start(out=both[:, own, :], in_=rows[:, own, :])
            for i in range(lo, hi):
                raw[c, i] = (both, lo * CHUNK)

        def raw_columns(raw, c, lo, hi):
            tile, first = raw[c, lo // CHUNK]
            return tile[:, :, lo - first:hi - first]

        def load_x(c, lo, hi, parts):
            load_columns("x", x, x_raw, c, lo, hi, parts)

        def load_w(c, lo, hi):
            load_columns("w", w, w_raw, c, lo, hi, 1)

        def load_bias():
            nc.sync.dma_start(out=bias_rows[0:P:BIAS_STEP, :], in_=b.rearrange("(t q i) o -> q t (i o)", t=TILES, i=QUAD))

        def turn_bias():
            nc.vector.transpose(out=bias[:], in_=bias_rows[:])

        def quantize_bb():
            quantize(bb_own[:, 0:P], bb_own[:, P:BB_WORDS].bitcast(U8), bb_bf[:])

        def swap_bb():
            nc.sync.dma_start(out=bb_far[0:SIDE, :].bitcast(I32), in_=bb_own[SIDE:P, :].bitcast(I32))
            nc.sync.dma_start(out=bb_far[SIDE:P, :].bitcast(I32), in_=bb_own[0:SIDE, :].bitcast(I32))

        def weave_a(copy, c):
            copy(out=a_bf[c][:].rearrange("p s d j -> p d s j"), in_=a_raw[c][:].rearrange("p j (d s) -> p d s j", s=PACK))

        def quantize_a(c):
            quantize(a_codes[c][:].rearrange("p s d -> p (s d)"), a_scales[c][:], a_bf[c][:].rearrange("p s d j -> p (s d) j"))

        def spread_a(c):
            for dst, src, width in ((win_codes[c], a_codes[c][:].bitcast(I32), QUAD),
                                    (win_scales[c], a_scales[c][:].bitcast(I32).rearrange("p (s i) -> p s i", s=PACK), QUAD // 4)):
                groups = dst[:, 0:PACK * P].bitcast(I32).rearrange("p (s q i) -> p s q i", q=QUADS, i=width)
                nc.vector.tensor_copy(out=groups[:, :, 2:QUADS, :], in_=src.unsqueeze(2).to_broadcast([P, PACK, 2, width]))

        def weave_x(copy, c, i, lo=0, hi=CHUNK):
            weave(copy, x_bf[c][:, i * CHUNK + lo:i * CHUNK + hi, :], raw_columns(x_raw, c, i * CHUNK + lo, i * CHUNK + hi))

        def share_x(c, i):
            weave_x(vec, c, i, 0, X_SHARE)
            weave_x(act, c, i, X_SHARE, CHUNK)

        def quantize_x(c, i):
            span = cols(i, i + 1)
            quantize(x_codes[c][:, span], x_scales[c][:, span], x_bf[c][:, span, :])

        def z_pass(c, i):
            h, side = divmod(i, 2)
            if h not in z_bank:
                z_bank[h] = whole_bank("z_bank%d" % h, 1 + h, [P, PACK, CHUNK])
            for s in range(PACK):
                at = s * P + (1 - side) * SIDE
                nc.tensor.matmul_mx(
                    out=z_bank[h][:, s, :],
                    lhsT=win_codes[c][:, at:at + P].bitcast(FP8X4), lhsT_scale=win_scales[c][:, at:at + P],
                    rhs=x_codes[c][:, cols(i, i + 1)].bitcast(FP8X4), rhs_scale=x_scales[c][:, cols(i, i + 1)],
                    start=(c == 0 and side == 0 and s == 0), stop=(c == PASSES - 1 and side == 1 and s == PACK - 1))

        def round_z(h):
            nc.scalar.copy(out=z_bf[h][:], in_=z_bank[h][:].rearrange("p s n -> p n s"))

        def quantize_z(h):
            quantize(z_codes[h][:], z_scales[h][:], z_bf[h][:])

        def low_product(h, q, u):
            rows = slice(QUAD * q, QUAD * (q + 1))
            src = bb_own if q // 2 == u else bb_far
            nc.tensor.matmul_mx(
                out=low_bank[q][:, cols(2 * h + u, 2 * h + u + 1)],
                lhsT=src[rows, 0:P].bitcast(FP8X4), lhsT_scale=src[rows, P:BB_WORDS].bitcast(U8),
                rhs=z_codes[h][rows, :].bitcast(FP8X4), rhs_scale=z_scales[h][rows, :],
                start=True, stop=True)

        def low_products(h, pair):
            for u in range(2):
                for q in (pair, pair + 2):
                    low_product(h, q, u)

        def copy_tile(copy, h, q, u):
            copy(out=low[q % 2][:, 2 * h + q // 2, u, :], in_=low_bank[q][:, cols(2 * h + u, 2 * h + u + 1)])

        def copy_bank(copy, h, q):
            copy(out=low[q % 2][:, 2 * h + q // 2, :, :].rearrange("p u n -> p (u n)"), in_=low_bank[q][:, cols(2 * h, 2 * h + 2)])

        def copy_low(h, pair):
            for q in (pair, pair + 2):
                copy_bank(act, h, q)

        def weave_w(copy, t, c, lo=0, hi=P):
            weave(copy, w_bf[t][:, c, lo:hi, :], raw_columns(w_raw, c, t * P + lo, t * P + hi))

        def quantize_w(t, c):
            quantize(w_codes[t][:, c * P:(c + 1) * P], w_scales[t][:, c * P:(c + 1) * P], w_bf[t][:, c, :, :])

        def main_pass(t, c, lo, hi, slot=None):
            if c == 0:
                y_bank[t, lo] = whole_bank("y_bank%d%d" % (t, lo), slot, [P, (hi - lo) * CHUNK])
            for i in range(lo, hi):
                nc.tensor.matmul_mx(
                    out=y_bank[t, lo][:, cols(i - lo, i - lo + 1)],
                    lhsT=w_codes[t][:, c * P:(c + 1) * P].bitcast(FP8X4), lhsT_scale=w_scales[t][:, c * P:(c + 1) * P],
                    rhs=x_codes[c][:, cols(i, i + 1)].bitcast(FP8X4), rhs_scale=x_scales[c][:, cols(i, i + 1)],
                    start=(c == 0 and i == lo), stop=(c == PASSES - 1 and i == hi - 1))

        def add(t, lo, hi, first=0):
            nc.vector.tensor_tensor(out=pre[t][:, cols(lo, hi)].rearrange("p (i n) -> p i n", n=CHUNK),
                                    in0=y_bank[t, first][:, cols(lo - first, hi - first)].rearrange("p (i n) -> p i n", n=CHUNK),
                                    in1=low[t // 2][:, lo:hi, t % 2, :], op=mybir.AluOpType.add)

        def squash(t, lo, hi):
            nc.scalar.activation(out=res[t][:, cols(lo, hi)], in_=pre[t][:, cols(lo, hi)], func=ACT.Tanh,
                                 bias=bias[:, BIAS_STEP * t:BIAS_STEP * t + 1])

        def store(t, lo, hi):
            nc.sync.dma_start(out=out[t * P:(t + 1) * P, cols(lo, hi)], in_=res[t][:, cols(lo, hi)])

        def finish(t, lo, hi):
            squash(t, lo, hi)
            store(t, lo, hi)

        nc.gpsimd.memset(bb_own[:, P:BB_WORDS].bitcast(I32), 0)
        for c in range(PASSES):
            nc.gpsimd.memset(a_scales[c][:].bitcast(I32), 0)
        nc.gpsimd.memset(bias_rows[:], 0.0)
        for c in range(PASSES):
            for win, width in ((win_codes[c], SIDE), (win_scales[c], SIDE // 4)):
                nc.vector.memset(win[:].bitcast(I32).rearrange("p (g i) -> p g i", i=width)[:, 0::2, :], 0)

        for q in (0, 2, 1, 3):
            load_bb(q)
        for c in range(PASSES):
            load_a(c)
        for c in range(PASSES):
            load_x(c, 0, CHUNKS, 1)
        weave(vec, bb_bf[:], bb_raw[:])
        weave_a(act, 1)
        quantize_bb()
        load_bias()
        load_w(0, 0, 3)
        swap_bb()
        load_w(1, 0, 2)
        load_w(1, 2, 3)
        load_w(0, 3, 4)
        load_w(1, 3, 4)

        weave_a(vec, 0)
        quantize_a(0)
        quantize_a(1)
        spread_a(0)
        spread_a(1)

        share_x(0, 0)
        share_x(0, 1)
        weave_x(act, 0, 3)
        quantize_x(0, 0)
        z_pass(0, 0)
        weave_x(vec, 0, 2)
        for i in range(1, CHUNKS):
            quantize_x(0, i)
            z_pass(0, i)
        share_x(1, 0)
        share_x(1, 1)
        weave_x(vec, 1, 2, 0, 56)
        weave_x(act, 1, 2, 56, 128)
        quantize_x(1, 0)
        z_pass(1, 0)
        quantize_x(1, 1)
        z_pass(1, 1)
        weave_x(vec, 1, 3, 0, 80)
        weave_x(act, 1, 3, 80, 128)
        quantize_x(1, 2)
        z_pass(1, 2)
        turn_bias()
        quantize_x(1, 3)
        z_pass(1, 3)
        round_z(0)
        round_z(1)
        weave_w(vec, 0, 0)
        weave_w(vec, 1, 0)
        quantize_w(0, 0)
        main_pass(0, 0, 0, 4, 3)
        weave_w(vec, 2, 0)
        quantize_z(0)
        for pair in range(2):
            low_products(0, pair)
        quantize_w(1, 0)
        main_pass(1, 0, 0, 4, 0)
        weave_w(vec, 0, 1)
        quantize_w(2, 0)
        weave_w(act, 1, 1)
        quantize_z(1)
        quantize_w(0, 1)
        main_pass(0, 1, 0, 4)
        copy_low(0, 0)
        for q in (0, 2):
            for u in range(2):
                low_product(1, q, u)
        copy_low(0, 1)
        weave_w(vec, 2, 1)
        quantize_w(1, 1)
        main_pass(1, 1, 0, 4)
        low_products(1, 1)
        main_pass(2, 0, 0, 4, 1)
        copy_low(1, 0)
        weave_w(vec, 3, 0)
        quantize_w(2, 1)
        main_pass(2, 1, 0, 4)
        add(0, 0, 2)
        quantize_w(3, 0)
        main_pass(3, 0, 0, 2, 2)
        finish(0, 0, 2)
        weave_w(vec, 3, 1)
        add(1, 0, 2)
        copy_low(1, 1)
        finish(1, 0, 2)
        add(0, 2, 4)
        quantize_w(3, 1)
        main_pass(3, 1, 0, 2)
        main_pass(3, 0, 2, 4, 3)
        main_pass(3, 1, 2, 4)
        add(1, 2, 4)
        finish(0, 2, 4)
        finish(1, 2, 4)
        for lo in (0, 2):
            add(2, lo, lo + 2)
            finish(2, lo, lo + 2)
        for lo in (0, 2):
            for i in (lo, lo + 1):
                add(3, i, i + 1, lo)
                squash(3, i, i + 1)
            store(3, lo, lo + 2)
